import numpy as np
import ml_dtypes


def mxq(x, axis, fmt="e4m3"):
    dtype, down = {"e4m3": (ml_dtypes.float8_e4m3fn, 7), "e5m2": (ml_dtypes.float8_e5m2, 14)}[fmt]
    v = np.moveaxis(np.asarray(x, np.float32).astype(ml_dtypes.bfloat16).astype(np.float64), axis, -1)
    blocks = v.reshape(v.shape[:-1] + (-1, 32))
    amax = np.abs(blocks).max(-1, keepdims=True)
    byte = np.maximum(np.where(amax > 0, np.frexp(amax)[1] - 1 + 127, 0) - down, 1)
    scale = np.exp2(byte - 127.0)
    codes = (blocks / scale).astype(np.float32).astype(dtype).astype(np.float64)
    return np.moveaxis((codes * scale).reshape(v.shape), -1, axis)


WIDE = False


def mx_kscale(k):
    if not WIDE:
        return np.ones(k)
    levels = np.array([10, -10, 5, -5, 0])
    if k % 512:
        return np.exp2(np.random.permutation(np.resize(levels, k // 32))).repeat(32)
    a = np.empty((k // 512, 16))
    for p in range(k // 512):
        a[p, :8] = np.random.permutation(np.resize(levels, 8))
        for g in range(8):
            far = levels[np.abs(levels - a[p, g]) >= 10]
            a[p, g + 8] = far[np.random.randint(len(far))]
    return np.exp2(a.ravel()).repeat(32)


BF16 = ml_dtypes.bfloat16


def bf(x):
    return np.asarray(x, np.float32).astype(BF16)


def f64(x):
    return np.asarray(x).astype(np.float64)


N, D, Z, ND = 1024, 1024, 512, 1024
DP = 2 * Z + ND
DQ = 2 * Z


def softplus(s):
    return np.maximum(s, 0.0) + np.log(1.0 + np.exp(-np.abs(s)))


def variance(r):
    return softplus(r) + 0.05


def draw0():
    s, u, t = mx_kscale(D), mx_kscale(D), mx_kscale(Z)
    return {
        "h": bf(np.random.standard_normal((N, D)) * s),
        "d": bf(np.random.standard_normal((N, D)) * u),
        "eps": bf(np.random.standard_normal((N, Z))),
        "wp": bf(np.random.standard_normal((D, DP)) * 1.5 / np.sqrt(D) / s[:, None]),
        "wq": bf(np.random.standard_normal((D, DQ)) * 1.5 / np.sqrt(D) / u[:, None]),
        "gz": bf((1.0 + 0.1 * np.random.standard_normal(Z)) * t),
        "wz": bf(np.random.standard_normal((Z, ND)) * 1.5 / np.sqrt(Z) / t[:, None]),
    }


def core(h, d, eps, wp, wq, gz, wz):
    nz = gz.shape[0]
    nd = wz.shape[1]

    pr = mxq(f64(h), 1, "e4m3") @ mxq(f64(wp), 0, "e4m3")
    mp = pr[:, :nz]
    rp = pr[:, nz:2 * nz]
    px = pr[:, 2 * nz:2 * nz + nd]

    en = mxq(f64(d), 1, "e4m3") @ mxq(f64(wq), 0, "e4m3")
    mh = en[:, :nz]
    rh = en[:, nz:2 * nz]

    vp = variance(rp)
    vh = variance(rh)

    vq = 1.0 / (1.0 / vh + 1.0 / vp)
    mq = (mh / vh + mp / vp) * vq

    z = (mq + np.sqrt(vq) * f64(eps)) * f64(gz)[None, :]

    return px + (mxq(z, 1, "e4m3") @ mxq(f64(wz), 0, "e4m3"))


def e4m3fn_bytes(y):
    return np.clip(np.asarray(y, np.float64), -448.0, 448.0).astype(np.float32).astype(ml_dtypes.float8_e4m3fn).view(np.uint8)


def e4m3fn_values(b):
    return np.asarray(b, np.uint8).view(ml_dtypes.float8_e4m3fn).astype(np.float64)


def setup_inputs():
    d = draw0()
    x0 = np.asarray(d['wp']).astype(np.float64)
    s = (np.max(np.abs(x0), axis=(1,), keepdims=True) / 448.0).astype(np.float32)
    out = {}
    for k, v in d.items():
        if k == 'wp':
            out['wp_bytes'] = e4m3fn_bytes(x0 / s.astype(np.float64))
            out['wp_scale'] = s
        else:
            out[k] = v
    return out


def reference(h, d, eps, wp_bytes, wp_scale, wq, gz, wz):
    return core(h, d, eps, e4m3fn_values(wp_bytes) * wp_scale.astype(np.float64), wq, gz, wz)

@@ -1,0 +1,617 @@
+from contextlib import ExitStack
+
+import concourse.mybir as mybir
+from concourse.masks import make_identity
+
+P = 128
+HALF = 512
+F32 = mybir.dt.float32
+BF16 = mybir.dt.bfloat16
+U32 = mybir.dt.uint32
+U8 = mybir.dt.uint8
+F8 = mybir.dt.float8_e4m3fn
+FP8X4 = mybir.dt.float8_e4m3fn_x4
+ACT = mybir.ActivationFunctionType
+ALU = mybir.AluOpType
+
+FLOPS = 2 * 1024 * 1024 * 3072 + 2 * 1024 * 512 * 1024
+VAR_MIN = 0.05
+LN_FLOOR = 2.0**-60
+
+
+def tile_laddertopdownprecisionmerge_kernel(tc, h, d, eps, wp_bytes, wp_scale, wq, gz, wz, out):
+    nc = tc.nc
+    with ExitStack() as ctx:
+        keep = ctx.enter_context(tc.tile_pool(name="keep", bufs=1))
+        work = ctx.enter_context(tc.tile_pool(name="work", bufs=1))
+        psum = ctx.enter_context(tc.psum_pool(name="psum", bufs=8))
+        ctx.enter_context(tc.manual_schedule())
+
+        def big(dtype, shape):
+            t = work.tile(shape, dtype, tag="big", name="big", bufs=14, align_bytes=64)
+            return t
+
+        def bank():
+            b = psum.tile([P, 512], F32, tag="bank", name="bank")
+            return b
+
+        warm = keep.tile([P, 1], F32)
+        nc.vector.memset(warm[:], 0.0)
+        nc.scalar.activation(out=warm[:], in_=warm[:], func=ACT.Sigmoid)
+        ident = keep.tile([P, P], F32)
+        make_identity(nc, ident[:])
+
+        wq_raw = {}
+        wp_raw = {}
+        rows_raw = {}
+        misc_raw = {}
+        scale = keep.tile([P, 8], F32)
+        neg_scale = keep.tile([P, 8], F32)
+        gz_bf = keep.tile([P, 4], BF16)
+        gain = keep.tile([P, 4], F32)
+
+        def load_wq(c, g):
+            if g not in wq_raw:
+                wq_raw[g] = big(BF16, [P, 4, 1024])
+            cols = slice(512 * c, 512 * c + 512)
+            nc.sync.dma_start(out=wq_raw[g][:, :, cols], in_=wq[512 * g : 512 * g + 512, cols].rearrange("(p j) n -> p j n", j=4))
+
+        def load_wp(part, g):
+            wp_raw[(part, g)] = keep.tile([P, 4, 1024], U8, name="wpb%d%d" % (part, g), align_bytes=64)
+            nc.sync.dma_start(
+                out=wp_raw[(part, g)][:],
+                in_=wp_bytes[512 * g : 512 * g + 512, 1024 * part : 1024 * part + 1024].rearrange("(p j) n -> p j n", j=4),
+            )
+
+        def load_rows(name, half, i):
+            if (name, half) not in rows_raw:
+                rows_raw[(name, half)] = big(BF16, [P, 4, 1024])
+            r0 = HALF * half + 256 * i
+            src = d if name == "d" else h
+            nc.sync.dma_start(
+                out=rows_raw[(name, half)][:, 2 * i : 2 * i + 2, :], in_=src[r0 : r0 + 256, :].rearrange("(r p) k -> p r k", p=P)
+            )
+
+        def load_scale():
+            nc.sync.dma_start(out=scale[:].rearrange("p (g t) -> p g t", g=2), in_=wp_scale.rearrange("(g p t) o -> p g (t o)", p=P, t=4))
+
+        def load_gain():
+            nc.sync.dma_start(out=gz_bf[:], in_=gz.rearrange("(p t) -> p t", t=4))
+
+        def load_eps():
+            misc_raw["eps"] = big(BF16, [P, 8, 512])
+            nc.sync.dma_start(out=misc_raw["eps"][:], in_=eps.rearrange("(r p) c -> p r c", p=P))
+
+        def load_wz():
+            misc_raw["wz"] = big(BF16, [P, 4, 1024])
+            nc.sync.dma_start(out=misc_raw["wz"][:], in_=wz.rearrange("(p j) n -> p j n", j=4))
+
+        def negate_scale():
+            nc.vector.tensor_scalar(out=neg_scale[:], in0=scale[:], scalar1=-1.0, scalar2=None, op0=ALU.mult)
+
+        def widen_gain():
+            nc.vector.tensor_copy(out=gain[:], in_=gz_bf[:])
+
+        codes = {}
+        scales = {}
+        grouped = {}
+
+        def quant(name, g):
+            key = (name, g)
+            codes[key] = keep.tile([P, 512], U32, name="codes_%s_%d" % key, align_bytes=64)
+            scales[key] = keep.tile([P, 512], U8, name="scales_%s_%d" % key, align_bytes=64)
+            nc.vector.quantize_mx(out=codes[key][:].bitcast(FP8X4), scales=scales[key][:], in_=grouped[key][:])
+
+        def new_grouped(key):
+            t = work.tile([P, 2048], BF16, tag="grouped", name="grouped", bufs=5, align_bytes=64)
+            grouped[key] = t
+            return t
+
+        def copy_out(engine, out_ap, in_ap):
+            if engine == "S":
+                nc.scalar.copy(out=out_ap, in_=in_ap)
+            else:
+                nc.vector.tensor_copy(out=out_ap, in_=in_ap)
+
+        def group_permuted(engine, key, src):
+            copy_out(
+                engine,
+                new_grouped(key)[:].rearrange("p (t m j) -> p t m j", t=4, j=4),
+                src.rearrange("p j (m t) -> p t m j", t=4),
+            )
+
+        def group_plain(engine, key, src):
+            copy_out(
+                engine,
+                new_grouped(key)[:].rearrange("p (c i j) -> p c j i", i=4, j=4),
+                src.rearrange("p j (c i) -> p c j i", i=4),
+            )
+
+        wide = {}
+
+        def widen(engine, part, c, g):
+            w = work.tile([P, 4, 512], BF16, tag="wide", name="wide", bufs=4, align_bytes=64)
+            wide[(part, c, g)] = w
+            sc = neg_scale if part == 0 else scale
+            for j in range(4):
+                src = wp_raw[(part, g)][:, j, 512 * c : 512 * c + 512].bitcast(F8)
+                s = sc[:, 4 * g + j : 4 * g + j + 1]
+                if engine == "S":
+                    nc.scalar.activation(out=w[:, j, :], in_=src, func=ACT.Copy, scale=s)
+                else:
+                    nc.vector.tensor_scalar(out=w[:, j, :], in0=src, scalar1=s, scalar2=None, op0=ALU.mult)
+
+        def group_q(engine, c, g):
+            group_permuted(engine, ("qm" if c == 0 else "qr", g), wq_raw[g][:, :, 512 * c : 512 * c + 512])
+
+        def group_p(engine, c, g):
+            group_permuted(engine, ("pm" if c == 0 else "pr", g), wide[(0, c, g)][:])
+
+        def group_x(engine, c, g):
+            group_plain(engine, ("x%d" % c, g), wide[(1, c, g)][:])
+
+        def group_w(engine, c):
+            group_plain(engine, ("w%d" % c, 0), misc_raw["wz"][:, :, 512 * c : 512 * c + 512])
+
+        turned = {}
+
+        def turn(name, half, g, i):
+            b = bank()
+            turned[(name, half, g, i)] = b
+            bv = b[:].rearrange("p (u n) -> p u n", u=2)
+            for r in range(2):
+                words = rows_raw[(name, half)][:, 2 * i + r, :].bitcast(F32)
+                for u in range(2):
+                    nc.tensor.transpose(bv[:, u, 128 * r : 128 * r + 128], words[:, 256 * g + u : 256 * (g + 1) : 2], ident[:])
+
+        def turn_out(engine, name, half, g, i):
+            key = ("%s%d" % (name, half), g)
+            grp = grouped[key] if key in grouped else new_grouped(key)
+            copy_out(
+                engine,
+                grp[:, 1024 * i : 1024 * i + 1024].bitcast(F32).rearrange("p (n u) -> p n u", u=2),
+                turned[(name, half, g, i)][:].rearrange("p (u n) -> p n u", u=2),
+            )
+
+        def mm(out_ap, lkey, lcols, rkey, start, stop):
+            nc.tensor.matmul_mx(
+                out=out_ap,
+                lhsT=codes[lkey][:, lcols].bitcast(FP8X4),
+                lhsT_scale=scales[lkey][:, lcols],
+                rhs=codes[rkey][:].bitcast(FP8X4),
+                rhs_scale=scales[rkey][:],
+                start=start,
+                stop=stop,
+            )
+
+        psums = {}
+
+        def channels(what, half, t):
+            dk, hk = "d%d" % half, "h%d" % half
+            terms = {"h": [("qr", dk)], "p": [("pr", hk)], "m": [("qm", dk)], "D": [("qm", dk), ("pm", hk)]}[what]
+            b = bank()
+            psums[(what, half, t)] = b
+            n = 2 * len(terms)
+            for i in range(n):
+                w, x = terms[i // 2]
+                mm(b[:], (w, i % 2), slice(128 * t, 128 * t + 128), (x, i % 2), i == 0, i == n - 1)
+
+        sg = {}
+        sp = {}
+
+        def sig(br, half, t):
+            if (br, half) not in sg:
+                sg[(br, half)] = big(F32, [P, 4, 512])
+            nc.scalar.activation(
+                out=sg[(br, half)][:, t, :], in_=psums[(br, half, t)][:], func=ACT.Sigmoid, scale=-1.0 if br == "h" else 1.0
+            )
+
+        def ln(br, half, t):
+            l = sg[(br, half)][:, t, :]
+            nc.scalar.activation(out=l, in_=l, func=ACT.Ln, bias=LN_FLOOR)
+
+        def softplus(br, half, t):
+            if (br, half) not in sp:
+                sp[(br, half)] = big(F32, [P, 4, 512])
+            l = sg[(br, half)][:, t, :]
+            o = sp[(br, half)][:, t, :]
+            s = psums[(br, half, t)]
+            if br == "h":
+                nc.vector.scalar_tensor_tensor(out=o, in0=l, scalar=-1.0, in1=s[:], op0=ALU.mult, op1=ALU.max)
+            else:
+                nc.vector.tensor_tensor(out=o, in0=l, in1=s[:], op=ALU.min)
+
+        def log_var(br, half, q):
+            ts = slice(2 * q, 2 * q + 2)
+            v = sp[(br, half)][:, ts, :]
+            o = v if br == "h" else sg[("p", half)][:, ts, :]
+            nc.scalar.activation(out=o, in_=v, func=ACT.Ln, bias=VAR_MIN, scale=1.0 if br == "h" else -1.0)
+
+        def log_ratio(half, q):
+            ts = slice(2 * q, 2 * q + 2)
+            vh = sp[("h", half)][:, ts, :]
+            nc.vector.tensor_tensor(out=vh, in0=vh, in1=sg[("p", half)][:, ts, :], op=ALU.subtract)
+
+        def weight(half, q):
+            w = sp[("h", half)][:, 2 * q : 2 * q + 2, :]
+            nc.scalar.activation(out=w, in_=w, func=ACT.Sigmoid)
+
+        def merged_var(half, q):
+            ts = slice(2 * q, 2 * q + 2)
+            nc.vector.scalar_tensor_tensor(
+                out=sg[("p", half)][:, ts, :],
+                in0=sp[("p", half)][:, ts, :],
+                scalar=VAR_MIN,
+                in1=sp[("h", half)][:, ts, :],
+                op0=ALU.subtract,
+                op1=ALU.mult,
+            )
+
+        def root(half, q):
+            v = sg[("p", half)][:, 2 * q : 2 * q + 2, :]
+            nc.scalar.activation(out=v, in_=v, func=ACT.Sqrt, scale=-1.0)
+
+        def shift(half, t):
+            nc.vector.scalar_tensor_tensor(
+                out=sg[("h", half)][:, t, :],
+                in0=sp[("h", half)][:, t, :],
+                scalar=gain[:, t : t + 1],
+                in1=psums[("D", half, t)][:],
+                op0=ALU.mult,
+                op1=ALU.mult,
+            )
+
+        def mean(half, t):
+            x = sg[("h", half)][:, t, :]
+            nc.vector.scalar_tensor_tensor(
+                out=x, in0=psums[("m", half, t)][:], scalar=gain[:, t : t + 1], in1=x, op0=ALU.mult, op1=ALU.subtract
+            )
+
+        def turn_eps(half, u):
+            b = bank()
+            psums[("eps", half, u)] = b
+            for r in range(4):
+                words = misc_raw["eps"][:, 4 * half + r, :].bitcast(F32)
+                nc.tensor.transpose(b[:, 128 * r : 128 * r + 128], words[:, u:256:2], ident[:])
+
+        def sample(half, t):
+            ev = psums[("eps", half, t // 2)][:].bitcast(BF16).rearrange("p (n e) -> p n e", e=2)[:, :, t % 2]
+            nc.vector.scalar_tensor_tensor(
+                out=sp[("p", half)][:, t, :], in0=sg[("p", half)][:, t, :], scalar=gain[:, t : t + 1], in1=ev, op0=ALU.mult, op1=ALU.mult
+            )
+
+        def latent(half, i):
+            key = ("z%d" % half, 0)
+            grp = grouped[key] if key in grouped else new_grouped(key)
+            n = slice(256 * i, 256 * i + 256)
+            nc.vector.tensor_tensor(
+                out=grp[:, 1024 * i : 1024 * i + 1024].rearrange("p (n t) -> p n t", t=4),
+                in0=sg[("h", half)][:, :, n].rearrange("p t n -> p n t"),
+                in1=sp[("p", half)][:, :, n].rearrange("p t n -> p n t"),
+                op=ALU.add,
+            )
+
+        def quant_z(half, i):
+            key = ("z%d" % half, 0)
+            if key not in codes:
+                codes[key] = keep.tile([P, 512], U32, name="codes_%s_%d" % key, align_bytes=64)
+                scales[key] = keep.tile([P, 512], U8, name="scales_%s_%d" % key, align_bytes=64)
+            n = slice(256 * i, 256 * i + 256)
+            nc.vector.quantize_mx(
+                out=codes[key][:, n].bitcast(FP8X4), scales=scales[key][:, n], in_=grouped[key][:, 1024 * i : 1024 * i + 1024]
+            )
+
+        def project_x(half, r, c):
+            b = bank()
+            psums[("o", half, r, c)] = b
+            for g in range(2):
+                mm(b[:], ("h%d" % half, g), slice(128 * r, 128 * r + 128), ("x%d" % c, g), g == 0, False)
+
+        def project_z(half, r, c):
+            mm(psums[("o", half, r, c)][:], ("z%d" % half, 0), slice(128 * r, 128 * r + 128), ("w%d" % c, 0), False, True)
+
+        o_tiles = {}
+
+        def finish(engine, half, r, c):
+            if (half, r) not in o_tiles:
+                o_tiles[(half, r)] = work.tile([P, 1024], F32, tag="out", name="o", bufs=3, align_bytes=64)
+            copy_out(engine, o_tiles[(half, r)][:, 512 * c : 512 * c + 512], psums[("o", half, r, c)][:])
+
+        def store(half, r):
+            r0 = HALF * half + 128 * r
+            nc.sync.dma_start(out=out[r0 : r0 + 128, :], in_=o_tiles[(half, r)][:])
+
+        load_scale()
+        load_wp(0, 1)
+        negate_scale()
+        load_wp(1, 0)
+        load_wp(0, 0)
+        load_wq(1, 1)
+        widen("V", 0, 0, 1)
+        widen("S", 0, 1, 1)
+        load_rows("h", 0, 1)
+        widen("V", 1, 0, 0)
+        group_p("S", 0, 1)
+        widen("V", 0, 1, 0)
+        load_wq(1, 0)
+        group_p("V", 1, 1)
+        load_rows("d", 0, 0)
+        turn("d", 0, 1, 0)
+        widen("V", 0, 0, 0)
+        group_q("S", 1, 1)
+        load_rows("h", 0, 0)
+        load_rows("d", 0, 1)
+        load_rows("d", 1, 0)
+        turn("h", 0, 0, 0)
+        load_rows("d", 1, 1)
+        group_p("S", 0, 0)
+        group_q("V", 1, 0)
+        quant("pr", 1)
+        turn("d", 0, 0, 0)
+        turn("d", 0, 0, 1)
+        quant("qr", 0)
+        turn("d", 0, 1, 1)
+        turn_out("S", "d", 0, 0, 0)
+        quant("pm", 1)
+        turn_out("S", "d", 0, 0, 1)
+        turn("d", 1, 1, 0)
+        turn("h", 0, 1, 1)
+        group_p("V", 1, 0)
+        load_rows("h", 1, 1)
+        quant("pm", 0)
+        turn("h", 0, 0, 1)
+        turn("d", 1, 0, 0)
+        turn_out("S", "d", 0, 1, 1)
+        turn("h", 0, 1, 0)
+        turn_out("S", "h", 0, 1, 1)
+        quant("pr", 0)
+        turn_out("S", "d", 0, 1, 0)
+        turn("d", 1, 1, 1)
+        quant("d0", 0)
+        turn_out("S", "h", 0, 0, 1)
+        turn("h", 1, 1, 1)
+        load_rows("h", 1, 0)
+        turn_out("S", "h", 0, 1, 0)
+        turn("h", 1, 1, 0)
+        quant("qr", 1)
+        widen("V", 1, 1, 0)
+        turn("h", 1, 0, 1)
+        quant("d0", 1)
+        quant("h0", 1)
+        turn("d", 1, 0, 1)
+        turn_out("S", "h", 0, 0, 0)
+        turn("h", 1, 0, 0)
+        load_wq(0, 1)
+        load_wp(1, 1)
+        turn_out("S", "h", 1, 1, 1)
+        turn_out("S", "h", 1, 1, 0)
+        channels("h", 0, 2)
+        turn_out("S", "h", 1, 0, 1)
+        quant("h0", 0)
+        turn_out("S", "d", 1, 1, 0)
+        turn_out("S", "d", 1, 1, 1)
+        widen("V", 1, 1, 1)
+        group_x("V", 0, 0)
+        turn_out("S", "d", 1, 0, 0)
+        turn_out("V", "d", 1, 0, 1)
+        channels("p", 0, 0)
+        turn_out("S", "h", 1, 0, 0)
+        quant("d1", 1)
+        quant("h1", 1)
+        channels("h", 0, 0)
+        channels("p", 0, 1)
+        channels("h", 0, 3)
+        quant("x0", 0)
+        channels("p", 0, 3)
+        quant("d1", 0)
+        sig("h", 0, 2)
+        sig("h", 0, 0)
+        sig("p", 0, 1)
+        channels("h", 0, 1)
+        sig("p", 0, 0)
+        load_wq(0, 0)
+        sig("p", 0, 3)
+        channels("p", 0, 2)
+        sig("h", 0, 1)
+        sig("h", 0, 3)
+        group_x("V", 1, 1)
+        load_wz()
+        sig("p", 0, 2)
+        group_w("V", 0)
+        ln("p", 0, 1)
+        ln("p", 0, 0)
+        ln("p", 0, 3)
+        ln("h", 0, 1)
+        group_q("V", 0, 0)
+        softplus("p", 0, 1)
+        ln("h", 0, 3)
+        ln("h", 0, 0)
+        ln("p", 0, 2)
+        softplus("p", 0, 0)
+        channels("h", 1, 0)
+        softplus("p", 0, 3)
+        quant("h1", 0)
+        log_var("p", 0, 0)
+        softplus("h", 0, 3)
+        channels("p", 1, 2)
+        load_gain()
+        channels("h", 1, 3)
+        channels("h", 1, 1)
+        softplus("h", 0, 1)
+        softplus("p", 0, 2)
+        log_var("p", 0, 1)
+        channels("p", 1, 3)
+        softplus("h", 0, 0)
+        group_w("V", 1)
+        group_q("V", 0, 1)
+        sig("p", 1, 2)
+        channels("p", 1, 1)
+        quant("w1", 0)
+        sig("h", 1, 0)
+        quant("x1", 1)
+        widen("V", 1, 0, 1)
+        group_x("V", 1, 0)
+        sig("h", 1, 1)
+        sig("h", 1, 3)
+        group_x("V", 0, 1)
+        quant("qm", 1)
+        sig("p", 1, 3)
+        ln("p", 1, 2)
+        ln("p", 1, 3)
+        quant("x1", 0)
+        ln("h", 0, 2)
+        softplus("h", 0, 2)
+        ln("h", 1, 1)
+        softplus("h", 1, 1)
+        ln("h", 1, 0)
+        quant("qm", 0)
+        softplus("p", 1, 2)
+        ln("h", 1, 3)
+        channels("h", 1, 2)
+        load_eps()
+        log_var("h", 0, 1)
+        softplus("h", 1, 0)
+        log_var("h", 0, 0)
+        log_ratio(0, 1)
+        quant("x0", 1)
+        sig("h", 1, 2)
+        softplus("h", 1, 3)
+        channels("D", 0, 3)
+        weight(0, 1)
+        turn_eps(0, 0)
+        log_ratio(0, 0)
+        quant("w0", 0)
+        weight(0, 0)
+        widen_gain()
+        channels("m", 0, 2)
+        softplus("p", 1, 3)
+        channels("D", 0, 0)
+        channels("p", 1, 0)
+        channels("D", 0, 2)
+        shift(0, 3)
+        channels("D", 0, 1)
+        shift(0, 0)
+        channels("m", 0, 1)
+        merged_var(0, 1)
+        sig("p", 1, 0)
+        sig("p", 1, 1)
+        root(0, 1)
+        shift(0, 2)
+        merged_var(0, 0)
+        channels("m", 0, 3)
+        shift(0, 1)
+        mean(0, 2)
+        turn_eps(0, 1)
+        root(0, 0)
+        mean(0, 3)
+        ln("p", 1, 1)
+        sample(0, 0)
+        channels("m", 0, 0)
+        sample(0, 2)
+        mean(0, 1)
+        ln("h", 1, 2)
+        channels("D", 1, 1)
+        project_x(0, 3, 1)
+        log_var("h", 1, 0)
+        mean(0, 0)
+        sample(0, 1)
+        softplus("p", 1, 1)
+        channels("D", 1, 3)
+        sample(0, 3)
+        softplus("h", 1, 2)
+        ln("p", 1, 0)
+        softplus("p", 1, 0)
+        latent(0, 1)
+        latent(0, 0)
+        log_var("p", 1, 1)
+        log_var("h", 1, 1)
+        log_var("p", 1, 0)
+        quant_z(0, 1)
+        log_ratio(1, 0)
+        project_x(0, 0, 0)
+        weight(1, 0)
+        log_ratio(1, 1)
+        project_x(0, 2, 0)
+        channels("m", 1, 1)
+        project_z(0, 3, 1)
+        channels("D", 1, 0)
+        project_x(0, 3, 0)
+        finish("S", 0, 3, 1)
+        quant_z(0, 0)
+        project_z(0, 3, 0)
+        project_z(0, 0, 0)
+        shift(1, 1)
+        project_z(0, 2, 0)
+        channels("D", 1, 2)
+        shift(1, 0)
+        merged_var(1, 0)
+        channels("m", 1, 0)
+        weight(1, 1)
+        finish("S", 0, 3, 0)
+        shift(1, 2)
+        mean(1, 1)
+        root(1, 0)
+        project_x(0, 1, 0)
+        project_x(0, 2, 1)
+        project_z(0, 1, 0)
+        channels("m", 1, 2)
+        channels("m", 1, 3)
+        store(0, 3)
+        shift(1, 3)
+        finish("S", 0, 1, 0)
+        merged_var(1, 1)
+        root(1, 1)
+        project_z(0, 2, 1)
+        turn_eps(1, 0)
+        turn_eps(1, 1)
+        mean(1, 2)
+        finish("S", 0, 0, 0)
+        mean(1, 0)
+        project_x(0, 1, 1)
+        finish("S", 0, 2, 1)
+        project_x(1, 2, 1)
+        mean(1, 3)
+        sample(1, 3)
+        sample(1, 1)
+        sample(1, 0)
+        project_x(1, 2, 0)
+        sample(1, 2)
+        finish("S", 0, 2, 0)
+        project_z(0, 1, 1)
+        project_x(0, 0, 1)
+        latent(1, 1)
+        project_z(0, 0, 1)
+        store(0, 2)
+        quant_z(1, 1)
+        finish("S", 0, 1, 1)
+        project_x(1, 0, 0)
+        project_x(1, 0, 1)
+        project_x(1, 3, 1)
+        finish("S", 0, 0, 1)
+        project_z(1, 2, 0)
+        finish("V", 1, 2, 0)
+        latent(1, 0)
+        project_z(1, 2, 1)
+        store(0, 1)
+        finish("S", 1, 2, 1)
+        project_z(1, 3, 1)
+        project_x(1, 3, 0)
+        project_z(1, 3, 0)
+        finish("S", 1, 3, 1)
+        project_x(1, 1, 1)
+        finish("S", 1, 3, 0)
+        quant_z(1, 0)
+        project_x(1, 1, 0)
+        project_z(1, 0, 1)
+        store(0, 0)
+        store(1, 2)
+        project_z(1, 0, 0)
+        project_z(1, 1, 0)
+        project_z(1, 1, 1)
+        finish("S", 1, 0, 0)
+        finish("S", 1, 1, 1)
+        store(1, 3)
+        finish("V", 1, 0, 1)
+        store(1, 0)
+        finish("V", 1, 1, 0)
+        store(1, 1)

@@ -28,7 +28,7 @@ def tile_laddertopdownprecisionmerge_kernel(tc, h, d, eps, wp_bytes, wp_scale, w
         ctx.enter_context(tc.manual_schedule())
 
         def big(dtype, shape):
-            t = work.tile(shape, dtype, tag="big", name="big", bufs=14, align_bytes=64)
+            t = work.tile(shape, dtype, tag="big", name="big", bufs=13, align_bytes=64)
             return t
 
         def bank():
@@ -50,26 +50,25 @@ def tile_laddertopdownprecisionmerge_kernel(tc, h, d, eps, wp_bytes, wp_scale, w
         gz_bf = keep.tile([P, 4], BF16)
         gain = keep.tile([P, 4], F32)
 
-        def load_wq(c, g):
-            if g not in wq_raw:
-                wq_raw[g] = big(BF16, [P, 4, 1024])
-            cols = slice(512 * c, 512 * c + 512)
-            nc.sync.dma_start(out=wq_raw[g][:, :, cols], in_=wq[512 * g : 512 * g + 512, cols].rearrange("(p j) n -> p j n", j=4))
+        def load_wq(g):
+            wq_raw[g] = big(BF16, [P, 4, 1024])
+            nc.sync.dma_start(out=wq_raw[g][:], in_=wq[512 * g : 512 * g + 512, :].rearrange("(p j) n -> p j n", j=4))
 
-        def load_wp(part, g):
-            wp_raw[(part, g)] = keep.tile([P, 4, 1024], U8, name="wpb%d%d" % (part, g), align_bytes=64)
+        def load_wp(g, jj):
+            if g not in wp_raw:
+                wp_raw[g] = keep.tile([P, 4, 2048], U8, name="wpb%d" % g, align_bytes=64)
             nc.sync.dma_start(
-                out=wp_raw[(part, g)][:],
-                in_=wp_bytes[512 * g : 512 * g + 512, 1024 * part : 1024 * part + 1024].rearrange("(p j) n -> p j n", j=4),
+                out=wp_raw[g][:, 2 * jj : 2 * jj + 2, :],
+                in_=wp_bytes[512 * g : 512 * g + 512, :].rearrange("(p j) n -> p j n", j=4)[:, 2 * jj : 2 * jj + 2, :],
             )
 
         def load_rows(name, half, i):
             if (name, half) not in rows_raw:
                 rows_raw[(name, half)] = big(BF16, [P, 4, 1024])
-            r0 = HALF * half + 256 * i
             src = d if name == "d" else h
             nc.sync.dma_start(
-                out=rows_raw[(name, half)][:, 2 * i : 2 * i + 2, :], in_=src[r0 : r0 + 256, :].rearrange("(r p) k -> p r k", p=P)
+                out=rows_raw[(name, half)][:, 2 * i : 2 * i + 2, :],
+                in_=src[HALF * half : HALF * half + HALF, :].rearrange("(p r) k -> p r k", r=4)[:, 2 * i : 2 * i + 2, :],
             )
 
         def load_scale():
@@ -78,9 +77,9 @@ def tile_laddertopdownprecisionmerge_kernel(tc, h, d, eps, wp_bytes, wp_scale, w
         def load_gain():
             nc.sync.dma_start(out=gz_bf[:], in_=gz.rearrange("(p t) -> p t", t=4))
 
-        def load_eps():
-            misc_raw["eps"] = big(BF16, [P, 8, 512])
-            nc.sync.dma_start(out=misc_raw["eps"][:], in_=eps.rearrange("(r p) c -> p r c", p=P))
+        def load_eps(half):
+            misc_raw[half] = work.tile([P, 4, 512], BF16, tag="eps", name="eps", bufs=2, align_bytes=64)
+            nc.sync.dma_start(out=misc_raw[half][:], in_=eps[HALF * half : HALF * half + HALF, :].rearrange("(p r) c -> p r c", r=4))
 
         def load_wz():
             misc_raw["wz"] = big(BF16, [P, 4, 1024])
@@ -116,8 +115,8 @@ def tile_laddertopdownprecisionmerge_kernel(tc, h, d, eps, wp_bytes, wp_scale, w
         def group_permuted(engine, key, src):
             copy_out(
                 engine,
-                new_grouped(key)[:].rearrange("p (t m j) -> p t m j", t=4, j=4),
-                src.rearrange("p j (m t) -> p t m j", t=4),
+                new_grouped(key)[:].rearrange("p (t m j) -> p m j t", t=4, j=4),
+                src.rearrange("p j (m t) -> p m j t", t=4),
             )
 
         def group_plain(engine, key, src):
@@ -134,7 +133,8 @@ def tile_laddertopdownprecisionmerge_kernel(tc, h, d, eps, wp_bytes, wp_scale, w
             wide[(part, c, g)] = w
             sc = neg_scale if part == 0 else scale
             for j in range(4):
-                src = wp_raw[(part, g)][:, j, 512 * c : 512 * c + 512].bitcast(F8)
+                c0 = 1024 * part + 512 * c
+                src = wp_raw[g][:, j, c0 : c0 + 512].bitcast(F8)
                 s = sc[:, 4 * g + j : 4 * g + j + 1]
                 if engine == "S":
                     nc.scalar.activation(out=w[:, j, :], in_=src, func=ACT.Copy, scale=s)
@@ -271,7 +271,7 @@ def tile_laddertopdownprecisionmerge_kernel(tc, h, d, eps, wp_bytes, wp_scale, w
             b = bank()
             psums[("eps", half, u)] = b
             for r in range(4):
-                words = misc_raw["eps"][:, 4 * half + r, :].bitcast(F32)
+                words = misc_raw[half][:, r, :].bitcast(F32)
                 nc.tensor.transpose(b[:, 128 * r : 128 * r + 128], words[:, u:256:2], ident[:])
 
         def sample(half, t):
@@ -285,9 +285,9 @@ def tile_laddertopdownprecisionmerge_kernel(tc, h, d, eps, wp_bytes, wp_scale, w
             grp = grouped[key] if key in grouped else new_grouped(key)
             n = slice(256 * i, 256 * i + 256)
             nc.vector.tensor_tensor(
-                out=grp[:, 1024 * i : 1024 * i + 1024].rearrange("p (n t) -> p n t", t=4),
-                in0=sg[("h", half)][:, :, n].rearrange("p t n -> p n t"),
-                in1=sp[("p", half)][:, :, n].rearrange("p t n -> p n t"),
+                out=grp[:, 1024 * i : 1024 * i + 1024].rearrange("p (n k t) -> p n t k", k=4, t=4),
+                in0=sg[("h", half)][:, :, n].rearrange("p t (n k) -> p n t k", k=4),
+                in1=sp[("p", half)][:, :, n].rearrange("p t (n k) -> p n t k", k=4),
                 op=ALU.add,
             )
 
@@ -318,300 +318,298 @@ def tile_laddertopdownprecisionmerge_kernel(tc, h, d, eps, wp_bytes, wp_scale, w
             copy_out(engine, o_tiles[(half, r)][:, 512 * c : 512 * c + 512], psums[("o", half, r, c)][:])
 
         def store(half, r):
-            r0 = HALF * half + 128 * r
-            nc.sync.dma_start(out=out[r0 : r0 + 128, :], in_=o_tiles[(half, r)][:])
+            nc.sync.dma_start(out=out[HALF * half : HALF * half + HALF, :].rearrange("(p r) n -> p r n", r=4)[:, r, :], in_=o_tiles[(half, r)][:])
 
-        load_scale()
-        load_wp(0, 1)
-        negate_scale()
-        load_wp(1, 0)
-        load_wp(0, 0)
-        load_wq(1, 1)
-        widen("V", 0, 0, 1)
-        widen("S", 0, 1, 1)
-        load_rows("h", 0, 1)
-        widen("V", 1, 0, 0)
-        group_p("S", 0, 1)
-        widen("V", 0, 1, 0)
-        load_wq(1, 0)
-        group_p("V", 1, 1)
-        load_rows("d", 0, 0)
-        turn("d", 0, 1, 0)
-        widen("V", 0, 0, 0)
-        group_q("S", 1, 1)
-        load_rows("h", 0, 0)
-        load_rows("d", 0, 1)
-        load_rows("d", 1, 0)
-        turn("h", 0, 0, 0)
-        load_rows("d", 1, 1)
-        group_p("S", 0, 0)
-        group_q("V", 1, 0)
-        quant("pr", 1)
-        turn("d", 0, 0, 0)
-        turn("d", 0, 0, 1)
-        quant("qr", 0)
-        turn("d", 0, 1, 1)
-        turn_out("S", "d", 0, 0, 0)
-        quant("pm", 1)
-        turn_out("S", "d", 0, 0, 1)
-        turn("d", 1, 1, 0)
-        turn("h", 0, 1, 1)
-        group_p("V", 1, 0)
-        load_rows("h", 1, 1)
-        quant("pm", 0)
-        turn("h", 0, 0, 1)
-        turn("d", 1, 0, 0)
-        turn_out("S", "d", 0, 1, 1)
-        turn("h", 0, 1, 0)
-        turn_out("S", "h", 0, 1, 1)
-        quant("pr", 0)
-        turn_out("S", "d", 0, 1, 0)
-        turn("d", 1, 1, 1)
-        quant("d0", 0)
-        turn_out("S", "h", 0, 0, 1)
-        turn("h", 1, 1, 1)
-        load_rows("h", 1, 0)
-        turn_out("S", "h", 0, 1, 0)
-        turn("h", 1, 1, 0)
+        load_wq(1)
+        load_wq(0)
+        group_q("V", 1, 1)
+        group_q("S", 0, 1)
         quant("qr", 1)
-        widen("V", 1, 1, 0)
-        turn("h", 1, 0, 1)
-        quant("d0", 1)
-        quant("h0", 1)
+        load_rows("d", 1, 1)
+        group_q("S", 1, 0)
+        load_rows("d", 1, 0)
         turn("d", 1, 0, 1)
-        turn_out("S", "h", 0, 0, 0)
-        turn("h", 1, 0, 0)
-        load_wq(0, 1)
-        load_wp(1, 1)
-        turn_out("S", "h", 1, 1, 1)
-        turn_out("S", "h", 1, 1, 0)
-        channels("h", 0, 2)
-        turn_out("S", "h", 1, 0, 1)
-        quant("h0", 0)
-        turn_out("S", "d", 1, 1, 0)
-        turn_out("S", "d", 1, 1, 1)
-        widen("V", 1, 1, 1)
-        group_x("V", 0, 0)
-        turn_out("S", "d", 1, 0, 0)
+        group_q("V", 0, 0)
+        load_wp(1, 0)
+        turn("d", 1, 1, 1)
+        quant("qm", 1)
+        turn("d", 1, 0, 0)
+        turn("d", 1, 1, 0)
         turn_out("V", "d", 1, 0, 1)
-        channels("p", 0, 0)
-        turn_out("S", "h", 1, 0, 0)
-        quant("d1", 1)
-        quant("h1", 1)
-        channels("h", 0, 0)
-        channels("p", 0, 1)
-        channels("h", 0, 3)
-        quant("x0", 0)
-        channels("p", 0, 3)
+        load_scale()
+        quant("qm", 0)
+        turn_out("S", "d", 1, 1, 1)
+        quant("qr", 0)
+        turn_out("S", "d", 1, 0, 0)
+        negate_scale()
+        load_wp(1, 1)
         quant("d1", 0)
-        sig("h", 0, 2)
-        sig("h", 0, 0)
-        sig("p", 0, 1)
-        channels("h", 0, 1)
-        sig("p", 0, 0)
-        load_wq(0, 0)
-        sig("p", 0, 3)
-        channels("p", 0, 2)
-        sig("h", 0, 1)
-        sig("h", 0, 3)
+        turn_out("S", "d", 1, 1, 0)
+        quant("d1", 1)
+        channels("h", 1, 2)
+        channels("h", 1, 0)
+        widen("V", 0, 0, 1)
+        load_rows("d", 0, 0)
+        widen("V", 0, 1, 1)
+        widen("S", 1, 1, 1)
+        channels("h", 1, 1)
+        channels("h", 1, 3)
+        load_rows("d", 0, 1)
+        sig("h", 1, 2)
+        group_p("V", 0, 1)
+        load_wp(0, 1)
+        group_p("V", 1, 1)
+        sig("h", 1, 1)
+        load_rows("h", 0, 0)
+        turn("d", 0, 1, 1)
+        turn("d", 0, 1, 0)
+        load_rows("h", 0, 1)
+        turn("d", 0, 0, 0)
+        turn_out("V", "d", 0, 1, 1)
+        load_rows("h", 1, 1)
+        sig("h", 1, 3)
+        load_rows("h", 1, 0)
+        sig("h", 1, 0)
+        turn("d", 0, 0, 1)
+        ln("h", 1, 1)
+        ln("h", 1, 0)
+        quant("pr", 1)
+        turn_out("S", "d", 0, 1, 0)
+        softplus("h", 1, 1)
+        turn_out("S", "d", 0, 0, 0)
+        turn("h", 0, 1, 1)
+        softplus("h", 1, 0)
+        quant("d0", 1)
+        quant("pm", 1)
+        turn("h", 0, 1, 0)
+        ln("h", 1, 2)
+        load_wp(0, 0)
         group_x("V", 1, 1)
+        turn("h", 1, 1, 1)
+        turn("h", 1, 0, 1)
+        turn_out("S", "h", 0, 1, 0)
+        turn_out("S", "d", 0, 0, 1)
+        quant("d0", 0)
+        turn_out("S", "h", 0, 1, 1)
+        turn("h", 1, 0, 0)
+        turn("h", 1, 1, 0)
+        channels("h", 0, 1)
+        load_gain()
+        softplus("h", 1, 2)
         load_wz()
-        sig("p", 0, 2)
+        widen("V", 0, 0, 0)
+        channels("h", 0, 2)
+        widen("V", 0, 1, 0)
+        channels("h", 0, 3)
+        turn_out("S", "h", 1, 1, 1)
+        turn_out("S", "h", 1, 0, 1)
+        turn("h", 0, 0, 1)
+        ln("h", 1, 3)
+        turn_out("V", "h", 1, 0, 0)
+        turn("h", 0, 0, 0)
+        log_var("h", 1, 0)
+        group_p("V", 1, 0)
+        sig("h", 0, 2)
+        quant("h1", 0)
+        channels("h", 0, 0)
+        turn_out("S", "h", 1, 1, 0)
+        sig("h", 0, 3)
+        quant("pr", 0)
+        quant("h1", 1)
+        group_w("V", 1)
+        channels("p", 1, 2)
+        sig("h", 0, 1)
+        softplus("h", 1, 3)
+        turn_out("S", "h", 0, 0, 0)
+        channels("p", 1, 1)
+        sig("h", 0, 0)
         group_w("V", 0)
+        widen("V", 1, 0, 0)
+        turn_out("S", "h", 0, 0, 1)
+        channels("p", 1, 3)
+        sig("p", 1, 2)
+        sig("p", 1, 1)
+        channels("p", 1, 0)
+        sig("p", 1, 3)
+        sig("p", 1, 0)
+        ln("h", 0, 3)
+        quant("h0", 0)
+        ln("p", 1, 1)
+        ln("p", 1, 2)
+        quant("h0", 1)
+        group_p("V", 0, 0)
+        ln("p", 1, 0)
+        softplus("p", 1, 1)
+        ln("h", 0, 1)
+        softplus("p", 1, 0)
+        group_x("V", 0, 0)
+        softplus("h", 0, 1)
+        ln("p", 1, 3)
+        softplus("h", 0, 3)
+        ln("h", 0, 0)
+        softplus("p", 1, 3)
+        log_var("p", 1, 0)
+        channels("p", 0, 1)
+        widen_gain()
+        ln("h", 0, 2)
+        channels("p", 0, 2)
+        softplus("p", 1, 2)
+        log_var("h", 1, 1)
+        sig("p", 0, 1)
+        channels("p", 0, 0)
+        quant("w1", 0)
+        sig("p", 0, 0)
+        channels("p", 0, 3)
+        log_ratio(1, 0)
+        widen("V", 1, 0, 1)
+        softplus("h", 0, 2)
+        weight(1, 0)
+        quant("w0", 0)
+        channels("m", 1, 1)
+        sig("p", 0, 2)
+        quant("pm", 0)
+        merged_var(1, 0)
+        channels("D", 1, 1)
+        channels("D", 1, 0)
+        load_eps(0)
+        load_eps(1)
+        sig("p", 0, 3)
+        softplus("h", 0, 0)
+        ln("p", 0, 3)
+        ln("p", 0, 2)
+        shift(1, 1)
+        channels("m", 1, 2)
+        turn_eps(0, 1)
         ln("p", 0, 1)
         ln("p", 0, 0)
-        ln("p", 0, 3)
-        ln("h", 0, 1)
-        group_q("V", 0, 0)
-        softplus("p", 0, 1)
-        ln("h", 0, 3)
-        ln("h", 0, 0)
-        ln("p", 0, 2)
-        softplus("p", 0, 0)
-        channels("h", 1, 0)
-        softplus("p", 0, 3)
-        quant("h1", 0)
-        log_var("p", 0, 0)
-        softplus("h", 0, 3)
-        channels("p", 1, 2)
-        load_gain()
-        channels("h", 1, 3)
-        channels("h", 1, 1)
-        softplus("h", 0, 1)
-        softplus("p", 0, 2)
-        log_var("p", 0, 1)
-        channels("p", 1, 3)
-        softplus("h", 0, 0)
-        group_w("V", 1)
-        group_q("V", 0, 1)
-        sig("p", 1, 2)
-        channels("p", 1, 1)
-        quant("w1", 0)
-        sig("h", 1, 0)
         quant("x1", 1)
-        widen("V", 1, 0, 1)
-        group_x("V", 1, 0)
-        sig("h", 1, 1)
-        sig("h", 1, 3)
-        group_x("V", 0, 1)
-        quant("qm", 1)
-        sig("p", 1, 3)
-        ln("p", 1, 2)
-        ln("p", 1, 3)
-        quant("x1", 0)
-        ln("h", 0, 2)
-        softplus("h", 0, 2)
-        ln("h", 1, 1)
-        softplus("h", 1, 1)
-        ln("h", 1, 0)
-        quant("qm", 0)
-        softplus("p", 1, 2)
-        ln("h", 1, 3)
-        channels("h", 1, 2)
-        load_eps()
-        log_var("h", 0, 1)
-        softplus("h", 1, 0)
         log_var("h", 0, 0)
-        log_ratio(0, 1)
-        quant("x0", 1)
-        sig("h", 1, 2)
-        softplus("h", 1, 3)
-        channels("D", 0, 3)
-        weight(0, 1)
-        turn_eps(0, 0)
-        log_ratio(0, 0)
-        quant("w0", 0)
-        weight(0, 0)
-        widen_gain()
-        channels("m", 0, 2)
-        softplus("p", 1, 3)
-        channels("D", 0, 0)
-        channels("p", 1, 0)
-        channels("D", 0, 2)
-        shift(0, 3)
-        channels("D", 0, 1)
-        shift(0, 0)
-        channels("m", 0, 1)
-        merged_var(0, 1)
-        sig("p", 1, 0)
-        sig("p", 1, 1)
-        root(0, 1)
-        shift(0, 2)
-        merged_var(0, 0)
-        channels("m", 0, 3)
-        shift(0, 1)
-        mean(0, 2)
-        turn_eps(0, 1)
-        root(0, 0)
-        mean(0, 3)
-        ln("p", 1, 1)
-        sample(0, 0)
-        channels("m", 0, 0)
-        sample(0, 2)
-        mean(0, 1)
-        ln("h", 1, 2)
-        channels("D", 1, 1)
-        project_x(0, 3, 1)
-        log_var("h", 1, 0)
-        mean(0, 0)
-        sample(0, 1)
-        softplus("p", 1, 1)
-        channels("D", 1, 3)
-        sample(0, 3)
-        softplus("h", 1, 2)
-        ln("p", 1, 0)
-        softplus("p", 1, 0)
-        latent(0, 1)
-        latent(0, 0)
+        group_x("V", 0, 1)
+        softplus("p", 0, 3)
+        softplus("p", 0, 2)
+        softplus("p", 0, 1)
         log_var("p", 1, 1)
-        log_var("h", 1, 1)
-        log_var("p", 1, 0)
-        quant_z(0, 1)
-        log_ratio(1, 0)
-        project_x(0, 0, 0)
-        weight(1, 0)
-        log_ratio(1, 1)
-        project_x(0, 2, 0)
-        channels("m", 1, 1)
-        project_z(0, 3, 1)
-        channels("D", 1, 0)
-        project_x(0, 3, 0)
-        finish("S", 0, 3, 1)
-        quant_z(0, 0)
-        project_z(0, 3, 0)
-        project_z(0, 0, 0)
-        shift(1, 1)
-        project_z(0, 2, 0)
-        channels("D", 1, 2)
-        shift(1, 0)
-        merged_var(1, 0)
+        softplus("p", 0, 0)
         channels("m", 1, 0)
-        weight(1, 1)
-        finish("S", 0, 3, 0)
-        shift(1, 2)
-        mean(1, 1)
-        root(1, 0)
-        project_x(0, 1, 0)
-        project_x(0, 2, 1)
-        project_z(0, 1, 0)
-        channels("m", 1, 2)
-        channels("m", 1, 3)
-        store(0, 3)
-        shift(1, 3)
-        finish("S", 0, 1, 0)
-        merged_var(1, 1)
-        root(1, 1)
-        project_z(0, 2, 1)
-        turn_eps(1, 0)
         turn_eps(1, 1)
-        mean(1, 2)
-        finish("S", 0, 0, 0)
+        log_var("h", 0, 1)
+        log_var("p", 0, 1)
+        quant("x0", 1)
+        channels("D", 0, 0)
+        log_var("p", 0, 0)
+        quant("x0", 0)
+        shift(1, 0)
+        log_ratio(1, 1)
+        weight(1, 1)
+        log_ratio(0, 1)
+        log_ratio(0, 0)
         mean(1, 0)
-        project_x(0, 1, 1)
-        finish("S", 0, 2, 1)
-        project_x(1, 2, 1)
-        mean(1, 3)
+        weight(0, 0)
+        weight(0, 1)
+        mean(1, 1)
+        merged_var(1, 1)
+        channels("D", 0, 3)
+        shift(0, 0)
+        channels("D", 0, 2)
+        channels("D", 1, 2)
+        root(1, 1)
+        channels("D", 1, 3)
+        shift(1, 2)
+        merged_var(0, 0)
+        root(1, 0)
+        shift(0, 2)
+        widen("S", 1, 1, 0)
+        shift(0, 3)
+        turn_eps(0, 0)
+        shift(1, 3)
+        channels("m", 1, 3)
+        channels("D", 0, 1)
+        turn_eps(1, 0)
+        group_x("S", 1, 0)
         sample(1, 3)
+        merged_var(0, 1)
+        mean(1, 2)
+        mean(1, 3)
         sample(1, 1)
+        channels("m", 0, 2)
         sample(1, 0)
-        project_x(1, 2, 0)
         sample(1, 2)
-        finish("S", 0, 2, 0)
-        project_z(0, 1, 1)
-        project_x(0, 0, 1)
+        shift(0, 1)
         latent(1, 1)
-        project_z(0, 0, 1)
-        store(0, 2)
+        channels("m", 0, 3)
+        channels("m", 0, 1)
+        project_x(1, 2, 0)
+        mean(0, 3)
         quant_z(1, 1)
-        finish("S", 0, 1, 1)
-        project_x(1, 0, 0)
-        project_x(1, 0, 1)
-        project_x(1, 3, 1)
-        finish("S", 0, 0, 1)
-        project_z(1, 2, 0)
-        finish("V", 1, 2, 0)
-        latent(1, 0)
-        project_z(1, 2, 1)
-        store(0, 1)
-        finish("S", 1, 2, 1)
-        project_z(1, 3, 1)
+        mean(0, 2)
         project_x(1, 3, 0)
+        quant("x1", 0)
+        root(0, 0)
+        channels("m", 0, 0)
         project_z(1, 3, 0)
-        finish("S", 1, 3, 1)
-        project_x(1, 1, 1)
+        root(0, 1)
+        project_z(1, 2, 0)
+        project_x(1, 0, 0)
+        finish("S", 1, 2, 0)
         finish("S", 1, 3, 0)
+        project_x(1, 3, 1)
+        project_z(1, 3, 1)
+        finish("S", 1, 3, 1)
+        mean(0, 1)
+        sample(0, 2)
+        project_x(1, 2, 1)
+        sample(0, 3)
+        latent(1, 0)
+        sample(0, 0)
+        project_x(0, 2, 1)
+        sample(0, 1)
+        project_z(1, 2, 1)
+        project_x(1, 1, 1)
+        project_x(0, 1, 1)
+        mean(0, 0)
+        project_x(0, 0, 1)
+        finish("S", 1, 2, 1)
         quant_z(1, 0)
-        project_x(1, 1, 0)
-        project_z(1, 0, 1)
-        store(0, 0)
-        store(1, 2)
-        project_z(1, 0, 0)
-        project_z(1, 1, 0)
-        project_z(1, 1, 1)
-        finish("S", 1, 0, 0)
-        finish("S", 1, 1, 1)
+        latent(0, 0)
         store(1, 3)
-        finish("V", 1, 0, 1)
+        project_x(1, 0, 1)
+        project_x(1, 1, 0)
+        project_z(1, 0, 0)
+        quant_z(0, 0)
+        project_z(1, 0, 1)
+        project_z(1, 1, 0)
+        project_x(0, 0, 0)
+        project_z(0, 0, 1)
+        finish("V", 0, 0, 1)
+        project_z(0, 0, 0)
+        project_z(0, 1, 1)
+        latent(0, 1)
+        finish("S", 1, 0, 0)
+        project_x(0, 1, 0)
+        project_z(0, 1, 0)
+        finish("S", 1, 0, 1)
+        store(1, 2)
+        project_x(0, 3, 1)
+        project_x(0, 3, 0)
+        finish("S", 0, 0, 0)
+        finish("S", 0, 1, 1)
+        quant_z(0, 1)
+        finish("S", 0, 1, 0)
+        project_z(1, 1, 1)
+        project_z(0, 2, 1)
         store(1, 0)
-        finish("V", 1, 1, 0)
+        project_z(0, 3, 0)
+        project_z(0, 3, 1)
+        store(0, 0)
+        finish("V", 1, 1, 1)
+        finish("S", 1, 1, 0)
+        project_x(0, 2, 0)
+        finish("V", 0, 3, 1)
+        project_z(0, 2, 0)
+        store(0, 1)
+        finish("V", 0, 2, 0)
         store(1, 1)
+        finish("S", 0, 2, 1)
+        finish("S", 0, 3, 0)
+        store(0, 3)
+        store(0, 2)

@@ -28,7 +28,7 @@ def tile_laddertopdownprecisionmerge_kernel(tc, h, d, eps, wp_bytes, wp_scale, w
         ctx.enter_context(tc.manual_schedule())
 
         def big(dtype, shape):
-            t = work.tile(shape, dtype, tag="big", name="big", bufs=13, align_bytes=64)
+            t = work.tile(shape, dtype, tag="big", name="big", bufs=15, align_bytes=64)
             return t
 
         def bank():
@@ -78,7 +78,7 @@ def tile_laddertopdownprecisionmerge_kernel(tc, h, d, eps, wp_bytes, wp_scale, w
             nc.sync.dma_start(out=gz_bf[:], in_=gz.rearrange("(p t) -> p t", t=4))
 
         def load_eps(half):
-            misc_raw[half] = work.tile([P, 4, 512], BF16, tag="eps", name="eps", bufs=2, align_bytes=64)
+            misc_raw[half] = big(BF16, [P, 4, 512])
             nc.sync.dma_start(out=misc_raw[half][:], in_=eps[HALF * half : HALF * half + HALF, :].rearrange("(p r) c -> p r c", r=4))
 
         def load_wz():
@@ -227,10 +227,9 @@ def tile_laddertopdownprecisionmerge_kernel(tc, h, d, eps, wp_bytes, wp_scale, w
             o = v if br == "h" else sg[("p", half)][:, ts, :]
             nc.scalar.activation(out=o, in_=v, func=ACT.Ln, bias=VAR_MIN, scale=1.0 if br == "h" else -1.0)
 
-        def log_ratio(half, q):
-            ts = slice(2 * q, 2 * q + 2)
+        def log_ratio(engine, half, ts):
             vh = sp[("h", half)][:, ts, :]
-            nc.vector.tensor_tensor(out=vh, in0=vh, in1=sg[("p", half)][:, ts, :], op=ALU.subtract)
+            (nc.gpsimd if engine == "G" else nc.vector).tensor_tensor(out=vh, in0=vh, in1=sg[("p", half)][:, ts, :], op=ALU.subtract)
 
         def weight(half, q):
             w = sp[("h", half)][:, 2 * q : 2 * q + 2, :]
@@ -280,11 +279,11 @@ def tile_laddertopdownprecisionmerge_kernel(tc, h, d, eps, wp_bytes, wp_scale, w
                 out=sp[("p", half)][:, t, :], in0=sg[("p", half)][:, t, :], scalar=gain[:, t : t + 1], in1=ev, op0=ALU.mult, op1=ALU.mult
             )
 
-        def latent(half, i):
+        def latent(engine, half, i):
             key = ("z%d" % half, 0)
             grp = grouped[key] if key in grouped else new_grouped(key)
             n = slice(256 * i, 256 * i + 256)
-            nc.vector.tensor_tensor(
+            (nc.gpsimd if engine == "G" else nc.vector).tensor_tensor(
                 out=grp[:, 1024 * i : 1024 * i + 1024].rearrange("p (n k t) -> p n t k", k=4, t=4),
                 in0=sg[("h", half)][:, :, n].rearrange("p t (n k) -> p n t k", k=4),
                 in1=sp[("p", half)][:, :, n].rearrange("p t (n k) -> p n t k", k=4),
@@ -314,302 +313,264 @@ def tile_laddertopdownprecisionmerge_kernel(tc, h, d, eps, wp_bytes, wp_scale, w
 
         def finish(engine, half, r, c):
             if (half, r) not in o_tiles:
-                o_tiles[(half, r)] = work.tile([P, 1024], F32, tag="out", name="o", bufs=3, align_bytes=64)
+                o_tiles[(half, r)] = big(F32, [P, 1024])
             copy_out(engine, o_tiles[(half, r)][:, 512 * c : 512 * c + 512], psums[("o", half, r, c)][:])
 
         def store(half, r):
             nc.sync.dma_start(out=out[HALF * half : HALF * half + HALF, :].rearrange("(p r) n -> p r n", r=4)[:, r, :], in_=o_tiles[(half, r)][:])
 
-        load_wq(1)
-        load_wq(0)
-        group_q("V", 1, 1)
-        group_q("S", 0, 1)
-        quant("qr", 1)
-        load_rows("d", 1, 1)
-        group_q("S", 1, 0)
-        load_rows("d", 1, 0)
-        turn("d", 1, 0, 1)
-        group_q("V", 0, 0)
-        load_wp(1, 0)
-        turn("d", 1, 1, 1)
-        quant("qm", 1)
-        turn("d", 1, 0, 0)
-        turn("d", 1, 1, 0)
-        turn_out("V", "d", 1, 0, 1)
+        def load_bytes(g):
+            for jj in range(2):
+                load_wp(g, jj)
+
+        def load_tokens(name, half):
+            for i in range(2):
+                load_rows(name, half, i)
+
+        def quant_rows(name):
+            for g in range(2):
+                quant(name, g)
+
+        def turn2(name, half, g):
+            for i in range(2):
+                turn(name, half, g, i)
+
+        def turn_out2(engine, name, half, g):
+            for i in range(2):
+                turn_out(engine, name, half, g, i)
+
+        def channels2(what, half, q):
+            for t in (2 * q, 2 * q + 1):
+                channels(what, half, t)
+
+        def sig2(br, half, q):
+            for t in (2 * q, 2 * q + 1):
+                sig(br, half, t)
+
+        def ln2(br, half, q):
+            for t in (2 * q, 2 * q + 1):
+                ln(br, half, t)
+
+        def softplus2(br, half, q):
+            for t in (2 * q, 2 * q + 1):
+                softplus(br, half, t)
+
+        def shift2(half, q):
+            for t in (2 * q, 2 * q + 1):
+                shift(half, t)
+
+        def mean2(half, q):
+            for t in (2 * q, 2 * q + 1):
+                mean(half, t)
+
+        def sample2(half, q):
+            for t in (2 * q, 2 * q + 1):
+                sample(half, t)
+
+        def project_x2(half, r):
+            for c in range(2):
+                project_x(half, r, c)
+
+        def project_z2(half, r):
+            for c in range(2):
+                project_z(half, r, c)
+
         load_scale()
-        quant("qm", 0)
-        turn_out("S", "d", 1, 1, 1)
-        quant("qr", 0)
-        turn_out("S", "d", 1, 0, 0)
         negate_scale()
-        load_wp(1, 1)
-        quant("d1", 0)
-        turn_out("S", "d", 1, 1, 0)
-        quant("d1", 1)
-        channels("h", 1, 2)
-        channels("h", 1, 0)
-        widen("V", 0, 0, 1)
-        load_rows("d", 0, 0)
-        widen("V", 0, 1, 1)
-        widen("S", 1, 1, 1)
-        channels("h", 1, 1)
-        channels("h", 1, 3)
-        load_rows("d", 0, 1)
-        sig("h", 1, 2)
-        group_p("V", 0, 1)
-        load_wp(0, 1)
-        group_p("V", 1, 1)
-        sig("h", 1, 1)
-        load_rows("h", 0, 0)
-        turn("d", 0, 1, 1)
-        turn("d", 0, 1, 0)
-        load_rows("h", 0, 1)
-        turn("d", 0, 0, 0)
-        turn_out("V", "d", 0, 1, 1)
-        load_rows("h", 1, 1)
-        sig("h", 1, 3)
-        load_rows("h", 1, 0)
-        sig("h", 1, 0)
-        turn("d", 0, 0, 1)
-        ln("h", 1, 1)
-        ln("h", 1, 0)
-        quant("pr", 1)
-        turn_out("S", "d", 0, 1, 0)
-        softplus("h", 1, 1)
-        turn_out("S", "d", 0, 0, 0)
-        turn("h", 0, 1, 1)
-        softplus("h", 1, 0)
-        quant("d0", 1)
-        quant("pm", 1)
-        turn("h", 0, 1, 0)
-        ln("h", 1, 2)
-        load_wp(0, 0)
-        group_x("V", 1, 1)
-        turn("h", 1, 1, 1)
-        turn("h", 1, 0, 1)
-        turn_out("S", "h", 0, 1, 0)
-        turn_out("S", "d", 0, 0, 1)
-        quant("d0", 0)
-        turn_out("S", "h", 0, 1, 1)
-        turn("h", 1, 0, 0)
-        turn("h", 1, 1, 0)
-        channels("h", 0, 1)
-        load_gain()
-        softplus("h", 1, 2)
-        load_wz()
-        widen("V", 0, 0, 0)
-        channels("h", 0, 2)
+        load_bytes(0)
         widen("V", 0, 1, 0)
-        channels("h", 0, 3)
-        turn_out("S", "h", 1, 1, 1)
-        turn_out("S", "h", 1, 0, 1)
-        turn("h", 0, 0, 1)
-        ln("h", 1, 3)
-        turn_out("V", "h", 1, 0, 0)
-        turn("h", 0, 0, 0)
-        log_var("h", 1, 0)
-        group_p("V", 1, 0)
-        sig("h", 0, 2)
-        quant("h1", 0)
-        channels("h", 0, 0)
-        turn_out("S", "h", 1, 1, 0)
-        sig("h", 0, 3)
-        quant("pr", 0)
-        quant("h1", 1)
-        group_w("V", 1)
-        channels("p", 1, 2)
-        sig("h", 0, 1)
-        softplus("h", 1, 3)
-        turn_out("S", "h", 0, 0, 0)
-        channels("p", 1, 1)
-        sig("h", 0, 0)
-        group_w("V", 0)
-        widen("V", 1, 0, 0)
-        turn_out("S", "h", 0, 0, 1)
-        channels("p", 1, 3)
-        sig("p", 1, 2)
-        sig("p", 1, 1)
-        channels("p", 1, 0)
-        sig("p", 1, 3)
-        sig("p", 1, 0)
-        ln("h", 0, 3)
-        quant("h0", 0)
-        ln("p", 1, 1)
-        ln("p", 1, 2)
-        quant("h0", 1)
-        group_p("V", 0, 0)
-        ln("p", 1, 0)
-        softplus("p", 1, 1)
-        ln("h", 0, 1)
-        softplus("p", 1, 0)
+        widen("V", 1, 1, 0)
+        load_tokens("d", 1)
+        load_wq(0)
+        turn2("d", 1, 1)
+        load_tokens("d", 0)
+        widen("S", 1, 0, 0)
+        turn2("d", 1, 0)
+        group_p("S", 1, 0)
+        turn2("d", 0, 1)
+        turn_out2("S", "d", 1, 1)
+        turn2("d", 0, 0)
+        load_wq(1)
         group_x("V", 0, 0)
-        softplus("h", 0, 1)
-        ln("p", 1, 3)
-        softplus("h", 0, 3)
-        ln("h", 0, 0)
-        softplus("p", 1, 3)
-        log_var("p", 1, 0)
-        channels("p", 0, 1)
-        widen_gain()
-        ln("h", 0, 2)
-        channels("p", 0, 2)
-        softplus("p", 1, 2)
-        log_var("h", 1, 1)
-        sig("p", 0, 1)
-        channels("p", 0, 0)
-        quant("w1", 0)
-        sig("p", 0, 0)
-        channels("p", 0, 3)
-        log_ratio(1, 0)
-        widen("V", 1, 0, 1)
-        softplus("h", 0, 2)
-        weight(1, 0)
-        quant("w0", 0)
-        channels("m", 1, 1)
-        sig("p", 0, 2)
-        quant("pm", 0)
-        merged_var(1, 0)
-        channels("D", 1, 1)
-        channels("D", 1, 0)
-        load_eps(0)
-        load_eps(1)
-        sig("p", 0, 3)
-        softplus("h", 0, 0)
-        ln("p", 0, 3)
-        ln("p", 0, 2)
-        shift(1, 1)
-        channels("m", 1, 2)
-        turn_eps(0, 1)
-        ln("p", 0, 1)
-        ln("p", 0, 0)
-        quant("x1", 1)
-        log_var("h", 0, 0)
-        group_x("V", 0, 1)
-        softplus("p", 0, 3)
-        softplus("p", 0, 2)
-        softplus("p", 0, 1)
-        log_var("p", 1, 1)
-        softplus("p", 0, 0)
-        channels("m", 1, 0)
-        turn_eps(1, 1)
-        log_var("h", 0, 1)
-        log_var("p", 0, 1)
-        quant("x0", 1)
-        channels("D", 0, 0)
-        log_var("p", 0, 0)
+        load_tokens("h", 0)
         quant("x0", 0)
-        shift(1, 0)
-        log_ratio(1, 1)
-        weight(1, 1)
-        log_ratio(0, 1)
-        log_ratio(0, 0)
-        mean(1, 0)
+        widen("S", 0, 0, 0)
+        load_bytes(1)
+        quant("pr", 0)
+        turn_out2("S", "d", 1, 0)
+        load_wz()
+        group_q("V", 1, 0)
+        group_q("V", 0, 0)
+        load_tokens("h", 1)
+        group_p("S", 0, 0)
+        quant("qr", 0)
+        turn_out2("S", "d", 0, 1)
+        load_gain()
+        quant("qm", 0)
+        quant_rows("d1")
+        turn2("h", 0, 1)
+        group_q("V", 1, 1)
+        turn_out2("S", "d", 0, 0)
+        quant("qr", 1)
+        turn_out2("S", "h", 0, 1)
+        group_q("V", 0, 1)
+        quant_rows("d0")
+        channels2("h", 1, 0)
+        turn2("h", 0, 0)
+        channels2("h", 0, 1)
+        quant("qm", 1)
+        widen("V", 0, 0, 1)
+        sig2("h", 1, 0)
+        group_x("V", 1, 0)
+        quant("pm", 0)
+        turn_out2("S", "h", 0, 0)
+        widen("V", 0, 1, 1)
+        sig2("h", 0, 1)
+        turn2("h", 1, 1)
+        widen("V", 1, 0, 1)
+        load_eps(0)
+        quant_rows("h0")
+        ln2("h", 0, 1)
+        group_p("V", 1, 1)
+        turn2("h", 1, 0)
+        turn_out2("S", "h", 1, 0)
+        widen("V", 1, 1, 1)
+        quant("pr", 1)
+        ln2("h", 1, 0)
+        channels2("h", 0, 0)
+        softplus2("h", 0, 1)
+        quant("x1", 0)
+        turn_out2("S", "h", 1, 1)
+        softplus2("h", 1, 0)
+        channels2("p", 0, 0)
+        sig2("p", 0, 0)
+        sig2("h", 0, 0)
+        load_eps(1)
+        channels2("p", 0, 1)
+        group_w("V", 1)
+        channels2("h", 1, 1)
+        sig2("p", 0, 1)
+        sig2("h", 1, 1)
+        group_w("V", 0)
+        ln2("h", 0, 0)
+        ln2("p", 0, 1)
+        group_p("V", 0, 1)
+        ln2("h", 1, 1)
+        quant_rows("h1")
+        ln2("p", 0, 0)
+        widen_gain()
+        softplus2("h", 0, 0)
+        group_x("V", 1, 1)
+        quant("pm", 1)
+        softplus2("p", 0, 1)
+        log_var("h", 0, 1)
+        softplus2("h", 1, 1)
+        channels2("p", 1, 1)
+        log_var("h", 0, 0)
+        softplus2("p", 0, 0)
+        channels2("D", 0, 0)
+        channels2("p", 1, 0)
+        log_var("p", 0, 1)
+        channels2("D", 0, 1)
+        quant("w0", 0)
+        log_ratio("V", 0, slice(2, 4))
+        log_var("p", 0, 0)
+        log_ratio("V", 0, slice(0, 2))
+        group_x("V", 0, 1)
+        log_var("h", 1, 1)
+        quant("x1", 1)
+        quant("w1", 0)
         weight(0, 0)
         weight(0, 1)
-        mean(1, 1)
-        merged_var(1, 1)
-        channels("D", 0, 3)
-        shift(0, 0)
-        channels("D", 0, 2)
-        channels("D", 1, 2)
-        root(1, 1)
-        channels("D", 1, 3)
-        shift(1, 2)
         merged_var(0, 0)
-        root(1, 0)
-        shift(0, 2)
-        widen("S", 1, 1, 0)
-        shift(0, 3)
-        turn_eps(0, 0)
-        shift(1, 3)
-        channels("m", 1, 3)
-        channels("D", 0, 1)
-        turn_eps(1, 0)
-        group_x("S", 1, 0)
-        sample(1, 3)
         merged_var(0, 1)
-        mean(1, 2)
-        mean(1, 3)
-        sample(1, 1)
-        channels("m", 0, 2)
-        sample(1, 0)
-        sample(1, 2)
-        shift(0, 1)
-        latent(1, 1)
-        channels("m", 0, 3)
-        channels("m", 0, 1)
-        project_x(1, 2, 0)
-        mean(0, 3)
-        quant_z(1, 1)
-        mean(0, 2)
-        project_x(1, 3, 0)
-        quant("x1", 0)
-        root(0, 0)
-        channels("m", 0, 0)
-        project_z(1, 3, 0)
+        sig2("p", 1, 0)
+        shift2(0, 0)
+        channels2("m", 0, 1)
+        sig2("p", 1, 1)
+        shift2(0, 1)
         root(0, 1)
-        project_z(1, 2, 0)
-        project_x(1, 0, 0)
-        finish("S", 1, 2, 0)
-        finish("S", 1, 3, 0)
-        project_x(1, 3, 1)
-        project_z(1, 3, 1)
-        finish("S", 1, 3, 1)
-        mean(0, 1)
-        sample(0, 2)
-        project_x(1, 2, 1)
-        sample(0, 3)
-        latent(1, 0)
-        sample(0, 0)
-        project_x(0, 2, 1)
-        sample(0, 1)
-        project_z(1, 2, 1)
-        project_x(1, 1, 1)
-        project_x(0, 1, 1)
-        mean(0, 0)
-        project_x(0, 0, 1)
-        finish("S", 1, 2, 1)
-        quant_z(1, 0)
-        latent(0, 0)
-        store(1, 3)
-        project_x(1, 0, 1)
-        project_x(1, 1, 0)
-        project_z(1, 0, 0)
-        quant_z(0, 0)
-        project_z(1, 0, 1)
-        project_z(1, 1, 0)
-        project_x(0, 0, 0)
-        project_z(0, 0, 1)
-        finish("V", 0, 0, 1)
-        project_z(0, 0, 0)
-        project_z(0, 1, 1)
-        latent(0, 1)
-        finish("S", 1, 0, 0)
-        project_x(0, 1, 0)
-        project_z(0, 1, 0)
-        finish("S", 1, 0, 1)
-        store(1, 2)
-        project_x(0, 3, 1)
-        project_x(0, 3, 0)
-        finish("S", 0, 0, 0)
-        finish("S", 0, 1, 1)
+        mean2(0, 1)
+        channels2("m", 0, 0)
+        root(0, 0)
+        turn_eps(0, 1)
+        quant("x0", 1)
+        mean2(0, 0)
+        ln2("p", 1, 0)
+        turn_eps(0, 0)
+        ln2("p", 1, 1)
+        sample2(0, 0)
+        sample2(0, 1)
+        softplus2("p", 1, 0)
+        softplus2("p", 1, 1)
+        latent("V", 0, 0)
+        channels2("D", 1, 0)
+        log_var("h", 1, 0)
+        log_var("p", 1, 0)
+        latent("V", 0, 1)
+        channels2("D", 1, 1)
+        log_var("p", 1, 1)
+        project_x2(0, 2)
+        log_ratio("V", 1, slice(0, 2))
+        project_x2(0, 3)
         quant_z(0, 1)
-        finish("S", 0, 1, 0)
-        project_z(1, 1, 1)
-        project_z(0, 2, 1)
-        store(1, 0)
-        project_z(0, 3, 0)
-        project_z(0, 3, 1)
-        store(0, 0)
-        finish("V", 1, 1, 1)
-        finish("S", 1, 1, 0)
-        project_x(0, 2, 0)
-        finish("V", 0, 3, 1)
-        project_z(0, 2, 0)
-        store(0, 1)
-        finish("V", 0, 2, 0)
-        store(1, 1)
-        finish("S", 0, 2, 1)
+        weight(1, 0)
+        project_z2(0, 3)
+        quant_z(0, 0)
+        log_ratio("V", 1, slice(2, 4))
+        shift2(1, 0)
+        project_z2(0, 2)
         finish("S", 0, 3, 0)
-        store(0, 3)
+        merged_var(1, 0)
+        weight(1, 1)
+        finish("S", 0, 2, 1)
+        turn_eps(1, 0)
+        project_x2(0, 1)
+        shift2(1, 1)
+        root(1, 0)
+        channels2("m", 1, 1)
+        mean2(1, 1)
+        merged_var(1, 1)
+        finish("S", 0, 2, 0)
+        project_z2(0, 1)
+        channels2("m", 1, 0)
+        project_x2(0, 0)
+        finish("S", 0, 3, 1)
+        sample2(1, 0)
+        turn_eps(1, 1)
+        mean2(1, 0)
+        project_x2(1, 2)
         store(0, 2)
+        root(1, 1)
+        sample2(1, 1)
+        finish("S", 0, 1, 1)
+        project_z2(0, 0)
+        latent("V", 1, 1)
+        finish("S", 0, 1, 0)
+        project_x2(1, 3)
+        finish("S", 0, 0, 0)
+        quant_z(1, 1)
+        latent("V", 1, 0)
+        project_x2(1, 1)
+        project_z2(1, 2)
+        project_z2(1, 3)
+        finish("V", 1, 2, 0)
+        finish("S", 0, 0, 1)
+        store(0, 1)
+        project_x2(1, 0)
+        quant_z(1, 0)
+        finish("S", 1, 2, 1)
+        store(0, 0)
+        store(0, 3)
+        finish("S", 1, 3, 0)
+        store(1, 2)
+        finish("V", 1, 3, 1)
+        project_z2(1, 1)
+        store(1, 3)
+        project_z2(1, 0)
+        finish("S", 1, 1, 1)
+        finish("V", 1, 1, 0)
+        finish("V", 1, 0, 0)
+        store(1, 1)
+        finish("S", 1, 0, 1)
+        store(1, 0)

@@ -1,3 +1,4 @@
+import math
 from contextlib import ExitStack
 
 import concourse.mybir as mybir
@@ -17,6 +18,7 @@ ALU = mybir.AluOpType
 FLOPS = 2 * 1024 * 1024 * 3072 + 2 * 1024 * 512 * 1024
 VAR_MIN = 0.05
 LN_FLOOR = 2.0**-60
+SHIFT = math.exp(-VAR_MIN)
 
 
 def tile_laddertopdownprecisionmerge_kernel(tc, h, d, eps, wp_bytes, wp_scale, wq, gz, wz, out):
@@ -54,12 +56,12 @@ def tile_laddertopdownprecisionmerge_kernel(tc, h, d, eps, wp_bytes, wp_scale, w
             wq_raw[g] = big(BF16, [P, 4, 1024])
             nc.sync.dma_start(out=wq_raw[g][:], in_=wq[512 * g : 512 * g + 512, :].rearrange("(p j) n -> p j n", j=4))
 
-        def load_wp(g, jj):
+        def load_wp(g, j0, j1):
             if g not in wp_raw:
                 wp_raw[g] = keep.tile([P, 4, 2048], U8, name="wpb%d" % g, align_bytes=64)
             nc.sync.dma_start(
-                out=wp_raw[g][:, 2 * jj : 2 * jj + 2, :],
-                in_=wp_bytes[512 * g : 512 * g + 512, :].rearrange("(p j) n -> p j n", j=4)[:, 2 * jj : 2 * jj + 2, :],
+                out=wp_raw[g][:, j0:j1, :],
+                in_=wp_bytes[512 * g : 512 * g + 512, :].rearrange("(p j) n -> p j n", j=4)[:, j0:j1, :],
             )
 
         def load_rows(name, half, i):
@@ -208,7 +210,10 @@ def tile_laddertopdownprecisionmerge_kernel(tc, h, d, eps, wp_bytes, wp_scale, w
 
         def ln(br, half, t):
             l = sg[(br, half)][:, t, :]
-            nc.scalar.activation(out=l, in_=l, func=ACT.Ln, bias=LN_FLOOR)
+            if br == "h":
+                nc.scalar.activation(out=l, in_=l, func=ACT.Ln, bias=LN_FLOOR)
+            else:
+                nc.scalar.activation(out=l, in_=l, func=ACT.Ln, bias=LN_FLOOR * SHIFT, scale=SHIFT)
 
         def softplus(br, half, t):
             if (br, half) not in sp:
@@ -219,32 +224,27 @@ def tile_laddertopdownprecisionmerge_kernel(tc, h, d, eps, wp_bytes, wp_scale, w
             if br == "h":
                 nc.vector.scalar_tensor_tensor(out=o, in0=l, scalar=-1.0, in1=s[:], op0=ALU.mult, op1=ALU.max)
             else:
-                nc.vector.tensor_tensor(out=o, in0=l, in1=s[:], op=ALU.min)
+                nc.vector.scalar_tensor_tensor(out=o, in0=s[:], scalar=VAR_MIN, in1=l, op0=ALU.subtract, op1=ALU.min)
 
         def log_var(br, half, q):
             ts = slice(2 * q, 2 * q + 2)
             v = sp[(br, half)][:, ts, :]
             o = v if br == "h" else sg[("p", half)][:, ts, :]
-            nc.scalar.activation(out=o, in_=v, func=ACT.Ln, bias=VAR_MIN, scale=1.0 if br == "h" else -1.0)
+            nc.scalar.activation(out=o, in_=v, func=ACT.Ln, bias=VAR_MIN if br == "h" else 0.0, scale=1.0 if br == "h" else -1.0)
 
-        def log_ratio(engine, half, ts):
-            vh = sp[("h", half)][:, ts, :]
-            (nc.gpsimd if engine == "G" else nc.vector).tensor_tensor(out=vh, in0=vh, in1=sg[("p", half)][:, ts, :], op=ALU.subtract)
+        def pick(engine):
+            return nc.gpsimd if engine == "G" else nc.vector
+
+        def log_ratio(engine, half, t):
+            vh = sp[("h", half)][:, t, :]
+            pick(engine).tensor_tensor(out=vh, in0=vh, in1=sg[("p", half)][:, t, :], op=ALU.subtract)
 
         def weight(half, q):
             w = sp[("h", half)][:, 2 * q : 2 * q + 2, :]
             nc.scalar.activation(out=w, in_=w, func=ACT.Sigmoid)
 
-        def merged_var(half, q):
-            ts = slice(2 * q, 2 * q + 2)
-            nc.vector.scalar_tensor_tensor(
-                out=sg[("p", half)][:, ts, :],
-                in0=sp[("p", half)][:, ts, :],
-                scalar=VAR_MIN,
-                in1=sp[("h", half)][:, ts, :],
-                op0=ALU.subtract,
-                op1=ALU.mult,
-            )
+        def merged_var(engine, half, t):
+            pick(engine).tensor_tensor(out=sg[("p", half)][:, t, :], in0=sp[("p", half)][:, t, :], in1=sp[("h", half)][:, t, :], op=ALU.mult)
 
         def root(half, q):
             v = sg[("p", half)][:, 2 * q : 2 * q + 2, :]
@@ -316,12 +316,19 @@ def tile_laddertopdownprecisionmerge_kernel(tc, h, d, eps, wp_bytes, wp_scale, w
                 o_tiles[(half, r)] = big(F32, [P, 1024])
             copy_out(engine, o_tiles[(half, r)][:, 512 * c : 512 * c + 512], psums[("o", half, r, c)][:])
 
-        def store(half, r):
-            nc.sync.dma_start(out=out[HALF * half : HALF * half + HALF, :].rearrange("(p r) n -> p r n", r=4)[:, r, :], in_=o_tiles[(half, r)][:])
+        def store(half, r, c):
+            n = slice(512 * c, 512 * c + 512)
+            nc.sync.dma_start(
+                out=out[HALF * half : HALF * half + HALF, n].rearrange("(p r) n -> p r n", r=4)[:, r, :], in_=o_tiles[(half, r)][:, n]
+            )
 
         def load_bytes(g):
-            for jj in range(2):
-                load_wp(g, jj)
+            if g == 0:
+                load_wp(0, 0, 1)
+                load_wp(0, 1, 2)
+            else:
+                load_wp(1, 0, 2)
+            load_wp(g, 2, 4)
 
         def load_tokens(name, half):
             for i in range(2):
@@ -378,199 +385,215 @@ def tile_laddertopdownprecisionmerge_kernel(tc, h, d, eps, wp_bytes, wp_scale, w
         load_scale()
         negate_scale()
         load_bytes(0)
-        widen("V", 0, 1, 0)
-        widen("V", 1, 1, 0)
-        load_tokens("d", 1)
-        load_wq(0)
-        turn2("d", 1, 1)
-        load_tokens("d", 0)
-        widen("S", 1, 0, 0)
-        turn2("d", 1, 0)
-        group_p("S", 1, 0)
-        turn2("d", 0, 1)
-        turn_out2("S", "d", 1, 1)
-        turn2("d", 0, 0)
-        load_wq(1)
-        group_x("V", 0, 0)
-        load_tokens("h", 0)
-        quant("x0", 0)
-        widen("S", 0, 0, 0)
-        load_bytes(1)
-        quant("pr", 0)
-        turn_out2("S", "d", 1, 0)
-        load_wz()
-        group_q("V", 1, 0)
-        group_q("V", 0, 0)
         load_tokens("h", 1)
+        widen("V", 0, 1, 0)
+        load_bytes(1)
+        group_p("V", 1, 0)
+        turn2("h", 1, 1)
+        widen("V", 1, 1, 0)
+        widen("S", 0, 0, 0)
+        quant("pr", 0)
+        widen("V", 0, 1, 1)
         group_p("S", 0, 0)
-        quant("qr", 0)
-        turn_out2("S", "d", 0, 1)
-        load_gain()
-        quant("qm", 0)
+        turn2("h", 1, 0)
+        load_tokens("d", 1)
+        turn_out2("S", "h", 1, 1)
+        load_wq(0)
+        quant("pm", 0)
+        turn2("d", 1, 1)
+        load_tokens("h", 0)
+        widen("S", 1, 1, 1)
+        widen("V", 0, 0, 1)
+        turn_out2("S", "h", 1, 0)
+        group_p("V", 1, 1)
+        widen("V", 1, 0, 1)
+        quant("pr", 1)
+        turn2("d", 1, 0)
+        quant_rows("h1")
+        channels2("p", 1, 0)
+        turn_out2("S", "d", 1, 1)
+        turn_out2("S", "d", 1, 0)
+        turn2("h", 0, 0)
+        group_q("V", 1, 0)
         quant_rows("d1")
+        load_tokens("d", 0)
         turn2("h", 0, 1)
+        group_q("V", 0, 0)
+        sig2("p", 1, 0)
+        turn2("d", 0, 1)
+        load_wq(1)
+        turn_out2("S", "h", 0, 0)
+        load_wz()
+        turn_out2("S", "h", 0, 1)
+        turn_out2("S", "d", 0, 1)
+        quant_rows("h0")
         group_q("V", 1, 1)
+        channels2("p", 1, 1)
+        turn2("d", 0, 0)
+        sig2("p", 1, 1)
+        quant("qr", 0)
+        channels2("p", 0, 1)
         turn_out2("S", "d", 0, 0)
         quant("qr", 1)
-        turn_out2("S", "h", 0, 1)
+        channels2("h", 1, 0)
+        group_w("V", 0)
+        group_x("V", 1, 1)
+        quant("qm", 0)
+        sig2("p", 0, 1)
+        sig2("h", 1, 0)
+        widen("V", 1, 0, 0)
+        ln2("h", 1, 0)
+        load_eps(1)
         group_q("V", 0, 1)
         quant_rows("d0")
-        channels2("h", 1, 0)
-        turn2("h", 0, 0)
-        channels2("h", 0, 1)
-        quant("qm", 1)
-        widen("V", 0, 0, 1)
-        sig2("h", 1, 0)
-        group_x("V", 1, 0)
-        quant("pm", 0)
-        turn_out2("S", "h", 0, 0)
-        widen("V", 0, 1, 1)
-        sig2("h", 0, 1)
-        turn2("h", 1, 1)
-        widen("V", 1, 0, 1)
-        load_eps(0)
-        quant_rows("h0")
-        ln2("h", 0, 1)
-        group_p("V", 1, 1)
-        turn2("h", 1, 0)
-        turn_out2("S", "h", 1, 0)
-        widen("V", 1, 1, 1)
-        quant("pr", 1)
-        ln2("h", 1, 0)
-        channels2("h", 0, 0)
-        softplus2("h", 0, 1)
-        quant("x1", 0)
-        turn_out2("S", "h", 1, 1)
         softplus2("h", 1, 0)
-        channels2("p", 0, 0)
-        sig2("p", 0, 0)
-        sig2("h", 0, 0)
-        load_eps(1)
-        channels2("p", 0, 1)
-        group_w("V", 1)
-        channels2("h", 1, 1)
-        sig2("p", 0, 1)
-        sig2("h", 1, 1)
-        group_w("V", 0)
-        ln2("h", 0, 0)
-        ln2("p", 0, 1)
-        group_p("V", 0, 1)
-        ln2("h", 1, 1)
-        quant_rows("h1")
-        ln2("p", 0, 0)
-        widen_gain()
-        softplus2("h", 0, 0)
-        group_x("V", 1, 1)
-        quant("pm", 1)
-        softplus2("p", 0, 1)
-        log_var("h", 0, 1)
-        softplus2("h", 1, 1)
-        channels2("p", 1, 1)
-        log_var("h", 0, 0)
-        softplus2("p", 0, 0)
-        channels2("D", 0, 0)
-        channels2("p", 1, 0)
-        log_var("p", 0, 1)
-        channels2("D", 0, 1)
-        quant("w0", 0)
-        log_ratio("V", 0, slice(2, 4))
-        log_var("p", 0, 0)
-        log_ratio("V", 0, slice(0, 2))
-        group_x("V", 0, 1)
-        log_var("h", 1, 1)
-        quant("x1", 1)
-        quant("w1", 0)
-        weight(0, 0)
-        weight(0, 1)
-        merged_var(0, 0)
-        merged_var(0, 1)
-        sig2("p", 1, 0)
-        shift2(0, 0)
-        channels2("m", 0, 1)
-        sig2("p", 1, 1)
-        shift2(0, 1)
-        root(0, 1)
-        mean2(0, 1)
-        channels2("m", 0, 0)
-        root(0, 0)
-        turn_eps(0, 1)
-        quant("x0", 1)
-        mean2(0, 0)
         ln2("p", 1, 0)
-        turn_eps(0, 0)
-        ln2("p", 1, 1)
-        sample2(0, 0)
-        sample2(0, 1)
+        channels2("p", 0, 0)
+        ln2("p", 0, 1)
         softplus2("p", 1, 0)
-        softplus2("p", 1, 1)
-        latent("V", 0, 0)
-        channels2("D", 1, 0)
+        group_x("V", 1, 0)
+        channels2("h", 0, 0)
+        ln2("p", 1, 1)
         log_var("h", 1, 0)
+        softplus2("p", 0, 1)
+        load_gain()
+        channels2("h", 1, 1)
+        softplus2("p", 1, 1)
+        quant("x1", 0)
         log_var("p", 1, 0)
-        latent("V", 0, 1)
-        channels2("D", 1, 1)
-        log_var("p", 1, 1)
-        project_x2(0, 2)
-        log_ratio("V", 1, slice(0, 2))
-        project_x2(0, 3)
-        quant_z(0, 1)
+        channels2("h", 0, 1)
+        log_ratio("G", 1, 0)
+        sig2("h", 1, 1)
+        sig2("h", 0, 1)
+        sig2("p", 0, 0)
+        log_ratio("V", 1, 1)
+        group_p("V", 0, 1)
+        group_x("V", 0, 1)
+        quant("qm", 1)
+        quant("x1", 1)
+        sig2("h", 0, 0)
+        group_w("V", 1)
         weight(1, 0)
-        project_z2(0, 3)
-        quant_z(0, 0)
-        log_ratio("V", 1, slice(2, 4))
-        shift2(1, 0)
-        project_z2(0, 2)
-        finish("S", 0, 3, 0)
-        merged_var(1, 0)
-        weight(1, 1)
-        finish("S", 0, 2, 1)
-        turn_eps(1, 0)
-        project_x2(0, 1)
-        shift2(1, 1)
-        root(1, 0)
-        channels2("m", 1, 1)
-        mean2(1, 1)
-        merged_var(1, 1)
-        finish("S", 0, 2, 0)
-        project_z2(0, 1)
+        ln2("h", 0, 0)
+        ln2("h", 1, 1)
+        group_x("V", 0, 0)
+        softplus2("h", 0, 0)
+        quant("w0", 0)
+        log_var("h", 0, 0)
+        quant("pm", 1)
+        log_var("p", 1, 1)
+        softplus2("h", 1, 1)
+        channels2("D", 1, 0)
+        merged_var("G", 1, 1)
+        ln2("p", 0, 0)
+        ln2("h", 0, 1)
+        quant("w1", 0)
+        channels2("D", 1, 1)
+        softplus2("p", 0, 0)
+        widen_gain()
+        quant("x0", 0)
+        merged_var("V", 1, 0)
+        softplus2("h", 0, 1)
         channels2("m", 1, 0)
-        project_x2(0, 0)
-        finish("S", 0, 3, 1)
-        sample2(1, 0)
+        log_var("h", 1, 1)
+        quant("x0", 1)
+        log_var("p", 0, 1)
+        log_var("p", 0, 0)
+        shift2(1, 0)
+        log_var("h", 0, 1)
+        log_ratio("G", 1, 3)
+        channels2("D", 0, 1)
+        log_ratio("V", 1, 2)
         turn_eps(1, 1)
+        log_ratio("V", 0, 3)
+        log_ratio("G", 0, 2)
         mean2(1, 0)
-        project_x2(1, 2)
-        store(0, 2)
+        weight(1, 1)
+        log_ratio("G", 0, 1)
+        shift2(1, 1)
+        log_ratio("G", 0, 0)
+        weight(0, 1)
+        shift2(0, 1)
+        merged_var("G", 1, 2)
+        weight(0, 0)
+        merged_var("G", 1, 3)
+        channels2("m", 0, 1)
+        mean2(0, 1)
+        root(1, 0)
+        channels2("D", 0, 0)
+        merged_var("G", 0, 0)
+        turn_eps(1, 0)
+        channels2("m", 1, 1)
+        shift2(0, 0)
+        mean2(1, 1)
+        merged_var("G", 0, 1)
+        merged_var("G", 0, 2)
+        channels2("m", 0, 0)
+        sample2(1, 0)
         root(1, 1)
+        load_eps(0)
+        project_x2(1, 2)
         sample2(1, 1)
-        finish("S", 0, 1, 1)
-        project_z2(0, 0)
-        latent("V", 1, 1)
-        finish("S", 0, 1, 0)
+        mean2(0, 0)
+        root(0, 0)
+        merged_var("G", 0, 3)
+        root(0, 1)
         project_x2(1, 3)
-        finish("S", 0, 0, 0)
-        quant_z(1, 1)
-        latent("V", 1, 0)
-        project_x2(1, 1)
-        project_z2(1, 2)
-        project_z2(1, 3)
-        finish("V", 1, 2, 0)
-        finish("S", 0, 0, 1)
-        store(0, 1)
+        turn_eps(0, 1)
+        turn_eps(0, 0)
+        latent("V", 1, 1)
         project_x2(1, 0)
-        quant_z(1, 0)
-        finish("S", 1, 2, 1)
-        store(0, 0)
-        store(0, 3)
+        quant_z(1, 1)
+        project_z2(1, 3)
+        latent("V", 1, 0)
+        project_z2(1, 2)
         finish("S", 1, 3, 0)
-        store(1, 2)
-        finish("V", 1, 3, 1)
-        project_z2(1, 1)
-        store(1, 3)
+        finish("S", 1, 2, 0)
+        quant_z(1, 0)
+        project_x2(1, 1)
         project_z2(1, 0)
+        project_z2(1, 1)
+        finish("S", 1, 3, 1)
+        sample2(0, 1)
+        project_x2(0, 0)
+        store(1, 2, 0)
+        sample2(0, 0)
+        latent("V", 0, 0)
+        finish("S", 1, 2, 1)
+        project_x2(0, 1)
+        store(1, 3, 1)
+        store(1, 3, 0)
+        finish("S", 1, 0, 0)
         finish("S", 1, 1, 1)
-        finish("V", 1, 1, 0)
-        finish("V", 1, 0, 0)
-        store(1, 1)
+        finish("S", 1, 1, 0)
+        quant_z(0, 0)
+        project_z2(0, 1)
+        latent("V", 0, 1)
+        finish("V", 0, 1, 1)
         finish("S", 1, 0, 1)
-        store(1, 0)
+        project_z2(0, 0)
+        quant_z(0, 1)
+        store(1, 0, 0)
+        finish("V", 0, 0, 1)
+        store(1, 1, 1)
+        store(1, 2, 1)
+        finish("S", 0, 1, 0)
+        store(1, 1, 0)
+        store(1, 0, 1)
+        store(0, 1, 0)
+        store(0, 1, 1)
+        finish("V", 0, 0, 0)
+        project_x2(0, 2)
+        project_z2(0, 2)
+        finish("V", 0, 2, 1)
+        store(0, 0, 1)
+        finish("V", 0, 2, 0)
+        store(0, 0, 0)
+        project_x2(0, 3)
+        project_z2(0, 3)
+        finish("V", 0, 3, 0)
+        store(0, 2, 1)
+        store(0, 2, 0)
+        store(0, 3, 0)
+        finish("V", 0, 3, 1)
+        store(0, 3, 1)

@@ -6,6 +6,7 @@ from concourse.masks import make_identity
 
 P = 128
 HALF = 512
+PASS = 512
 F32 = mybir.dt.float32
 BF16 = mybir.dt.bfloat16
 U32 = mybir.dt.uint32
@@ -18,7 +19,8 @@ ALU = mybir.AluOpType
 FLOPS = 2 * 1024 * 1024 * 3072 + 2 * 1024 * 512 * 1024
 VAR_MIN = 0.05
 LN_FLOOR = 2.0**-60
-SHIFT = math.exp(-VAR_MIN)
+LN_SCALE = math.exp(-VAR_MIN)
+FIRST_COLUMN = {"mp": 0, "rp": 512, "px0": 1024, "px1": 1536, "mh": 0, "rh": 512, "wz0": 0, "wz1": 512}
 
 
 def tile_laddertopdownprecisionmerge_kernel(tc, h, d, eps, wp_bytes, wp_scale, wq, gz, wz, out):
@@ -29,571 +31,525 @@ def tile_laddertopdownprecisionmerge_kernel(tc, h, d, eps, wp_bytes, wp_scale, w
         psum = ctx.enter_context(tc.psum_pool(name="psum", bufs=8))
         ctx.enter_context(tc.manual_schedule())
 
-        def big(dtype, shape):
-            t = work.tile(shape, dtype, tag="big", name="big", bufs=15, align_bytes=64)
-            return t
-
-        def bank():
-            b = psum.tile([P, 512], F32, tag="bank", name="bank")
-            return b
-
-        warm = keep.tile([P, 1], F32)
-        nc.vector.memset(warm[:], 0.0)
-        nc.scalar.activation(out=warm[:], in_=warm[:], func=ACT.Sigmoid)
+        first = keep.tile([P, 1], F32)
+        nc.vector.memset(first[:], 0.0)
+        nc.scalar.activation(out=first[:], in_=first[:], func=ACT.Sigmoid)
         ident = keep.tile([P, P], F32)
         make_identity(nc, ident[:])
 
-        wq_raw = {}
-        wp_raw = {}
-        rows_raw = {}
-        misc_raw = {}
         scale = keep.tile([P, 8], F32)
         neg_scale = keep.tile([P, 8], F32)
-        gz_bf = keep.tile([P, 4], BF16)
+        gain_bf16 = keep.tile([P, 4], BF16)
         gain = keep.tile([P, 4], F32)
 
-        def load_wq(g):
-            wq_raw[g] = big(BF16, [P, 4, 1024])
-            nc.sync.dma_start(out=wq_raw[g][:], in_=wq[512 * g : 512 * g + 512, :].rearrange("(p j) n -> p j n", j=4))
-
-        def load_wp(g, j0, j1):
-            if g not in wp_raw:
-                wp_raw[g] = keep.tile([P, 4, 2048], U8, name="wpb%d" % g, align_bytes=64)
-            nc.sync.dma_start(
-                out=wp_raw[g][:, j0:j1, :],
-                in_=wp_bytes[512 * g : 512 * g + 512, :].rearrange("(p j) n -> p j n", j=4)[:, j0:j1, :],
-            )
-
-        def load_rows(name, half, i):
-            if (name, half) not in rows_raw:
-                rows_raw[(name, half)] = big(BF16, [P, 4, 1024])
-            src = d if name == "d" else h
-            nc.sync.dma_start(
-                out=rows_raw[(name, half)][:, 2 * i : 2 * i + 2, :],
-                in_=src[HALF * half : HALF * half + HALF, :].rearrange("(p r) k -> p r k", r=4)[:, 2 * i : 2 * i + 2, :],
-            )
-
-        def load_scale():
-            nc.sync.dma_start(out=scale[:].rearrange("p (g t) -> p g t", g=2), in_=wp_scale.rearrange("(g p t) o -> p g (t o)", p=P, t=4))
-
-        def load_gain():
-            nc.sync.dma_start(out=gz_bf[:], in_=gz.rearrange("(p t) -> p t", t=4))
-
-        def load_eps(half):
-            misc_raw[half] = big(BF16, [P, 4, 512])
-            nc.sync.dma_start(out=misc_raw[half][:], in_=eps[HALF * half : HALF * half + HALF, :].rearrange("(p r) c -> p r c", r=4))
-
-        def load_wz():
-            misc_raw["wz"] = big(BF16, [P, 4, 1024])
-            nc.sync.dma_start(out=misc_raw["wz"][:], in_=wz.rearrange("(p j) n -> p j n", j=4))
-
-        def negate_scale():
-            nc.vector.tensor_scalar(out=neg_scale[:], in0=scale[:], scalar1=-1.0, scalar2=None, op0=ALU.mult)
-
-        def widen_gain():
-            nc.vector.tensor_copy(out=gain[:], in_=gz_bf[:])
-
+        raw = {}
+        wp_codes = {}
+        wide = {}
+        grouped = {}
         codes = {}
         scales = {}
-        grouped = {}
+        banks = {}
+        work_a = {}
+        work_b = {}
+        rows_out = {}
 
-        def quant(name, g):
-            key = (name, g)
-            codes[key] = keep.tile([P, 512], U32, name="codes_%s_%d" % key, align_bytes=64)
-            scales[key] = keep.tile([P, 512], U8, name="scales_%s_%d" % key, align_bytes=64)
-            nc.vector.quantize_mx(out=codes[key][:].bitcast(FP8X4), scales=scales[key][:], in_=grouped[key][:])
+        def new_slot(shape, dtype):
+            tile = work.tile(shape, dtype, tag="slot", name="slot", bufs=15, align_bytes=64)
+            return tile
 
         def new_grouped(key):
-            t = work.tile([P, 2048], BF16, tag="grouped", name="grouped", bufs=5, align_bytes=64)
-            grouped[key] = t
-            return t
+            tile = work.tile([P, 4 * PASS], BF16, tag="grouped", name="grouped", bufs=5, align_bytes=64)
+            grouped[key] = tile
+            return tile
 
-        def copy_out(engine, out_ap, in_ap):
+        def new_bank():
+            tile = psum.tile([P, 512], F32, tag="bank", name="bank")
+            return tile
+
+        def new_codes(key):
+            codes[key] = keep.tile([P, PASS], U32, name="codes_%s_%d" % key, align_bytes=64)
+            scales[key] = keep.tile([P, PASS], U8, name="scales_%s_%d" % key, align_bytes=64)
+
+        def copy(engine, out_ap, in_ap):
             if engine == "S":
                 nc.scalar.copy(out=out_ap, in_=in_ap)
             else:
                 nc.vector.tensor_copy(out=out_ap, in_=in_ap)
 
-        def group_permuted(engine, key, src):
-            copy_out(
-                engine,
-                new_grouped(key)[:].rearrange("p (t m j) -> p m j t", t=4, j=4),
-                src.rearrange("p j (m t) -> p m j t", t=4),
+        def vector_or_gpsimd(engine):
+            return nc.gpsimd if engine == "G" else nc.vector
+        def load_scale():
+            nc.sync.dma_start(
+                out=scale[:].rearrange("p (g j) -> p g j", g=2), in_=wp_scale.rearrange("(g p j) o -> p g (j o)", p=P, j=4)
             )
 
-        def group_plain(engine, key, src):
-            copy_out(
-                engine,
-                new_grouped(key)[:].rearrange("p (c i j) -> p c j i", i=4, j=4),
-                src.rearrange("p j (c i) -> p c j i", i=4),
+        def load_gain():
+            nc.sync.dma_start(out=gain_bf16[:], in_=gz.rearrange("(p t) -> p t", t=4))
+
+        def load_bytes(g):
+            wp_codes[g] = keep.tile([P, 4, 2048], U8, name="wp_codes_%d" % g, align_bytes=64)
+            rows = wp_bytes[PASS * g : PASS * g + PASS, :].rearrange("(p j) n -> p j n", j=4)
+            for j0, j1 in ((0, 1), (1, 2), (2, 4)) if g == 0 else ((0, 2), (2, 4)):
+                nc.sync.dma_start(out=wp_codes[g][:, j0:j1, :], in_=rows[:, j0:j1, :])
+
+        def load_tokens(name, half):
+            raw[(name, half)] = new_slot([P, 4, 1024], BF16)
+            rows = (d if name == "d" else h)[HALF * half : HALF * half + HALF, :].rearrange("(p r) k -> p r k", r=4)
+            for i in range(2):
+                nc.sync.dma_start(out=raw[(name, half)][:, 2 * i : 2 * i + 2, :], in_=rows[:, 2 * i : 2 * i + 2, :])
+
+        def load_wq(g):
+            raw[("wq", g)] = new_slot([P, 4, 1024], BF16)
+            nc.sync.dma_start(out=raw[("wq", g)][:], in_=wq[PASS * g : PASS * g + PASS, :].rearrange("(p j) n -> p j n", j=4))
+
+        def load_wz():
+            raw["wz"] = new_slot([P, 4, 1024], BF16)
+            nc.sync.dma_start(out=raw["wz"][:], in_=wz.rearrange("(p j) n -> p j n", j=4))
+
+        def load_eps(half):
+            raw[("eps", half)] = new_slot([P, 4, 512], BF16)
+            nc.sync.dma_start(
+                out=raw[("eps", half)][:], in_=eps[HALF * half : HALF * half + HALF, :].rearrange("(p r) c -> p r c", r=4)
             )
 
-        wide = {}
+        def negate_scale():
+            nc.vector.tensor_scalar(out=neg_scale[:], in0=scale[:], scalar1=-1.0, scalar2=None, op0=ALU.mult)
 
-        def widen(engine, part, c, g):
-            w = work.tile([P, 4, 512], BF16, tag="wide", name="wide", bufs=4, align_bytes=64)
-            wide[(part, c, g)] = w
-            sc = neg_scale if part == 0 else scale
+        def widen_gain():
+            nc.vector.tensor_copy(out=gain[:], in_=gain_bf16[:])
+
+        def widen(engine, name, g):
+            wide[(name, g)] = work.tile([P, 4, 512], BF16, tag="wide", name="wide", bufs=4, align_bytes=64)
+            factors = neg_scale if name in ("mp", "rp") else scale
+            first = FIRST_COLUMN[name]
             for j in range(4):
-                c0 = 1024 * part + 512 * c
-                src = wp_raw[g][:, j, c0 : c0 + 512].bitcast(F8)
-                s = sc[:, 4 * g + j : 4 * g + j + 1]
+                values = wp_codes[g][:, j, first : first + 512].bitcast(F8)
+                factor = factors[:, 4 * g + j : 4 * g + j + 1]
                 if engine == "S":
-                    nc.scalar.activation(out=w[:, j, :], in_=src, func=ACT.Copy, scale=s)
+                    nc.scalar.activation(out=wide[(name, g)][:, j, :], in_=values, func=ACT.Copy, scale=factor)
                 else:
-                    nc.vector.tensor_scalar(out=w[:, j, :], in0=src, scalar1=s, scalar2=None, op0=ALU.mult)
+                    nc.vector.tensor_scalar(out=wide[(name, g)][:, j, :], in0=values, scalar1=factor, scalar2=None, op0=ALU.mult)
 
-        def group_q(engine, c, g):
-            group_permuted(engine, ("qm" if c == 0 else "qr", g), wq_raw[g][:, :, 512 * c : 512 * c + 512])
+        def lay_out(engine, name, g):
+            if name in ("mh", "rh"):
+                rows = raw[("wq", g)][:, :, FIRST_COLUMN[name] : FIRST_COLUMN[name] + 512]
+            elif name in ("wz0", "wz1"):
+                rows = raw["wz"][:, :, FIRST_COLUMN[name] : FIRST_COLUMN[name] + 512]
+            else:
+                rows = wide[(name, g)][:]
+            words = new_grouped((name, g))
+            if name in ("mp", "rp", "mh", "rh"):
+                copy(engine, words[:].rearrange("p (t m j) -> p m j t", t=4, j=4), rows.rearrange("p j (m t) -> p m j t", t=4))
+            else:
+                copy(engine, words[:].rearrange("p (n i j) -> p n j i", i=4, j=4), rows.rearrange("p j (n i) -> p n j i", i=4))
 
-        def group_p(engine, c, g):
-            group_permuted(engine, ("pm" if c == 0 else "pr", g), wide[(0, c, g)][:])
-
-        def group_x(engine, c, g):
-            group_plain(engine, ("x%d" % c, g), wide[(1, c, g)][:])
-
-        def group_w(engine, c):
-            group_plain(engine, ("w%d" % c, 0), misc_raw["wz"][:, :, 512 * c : 512 * c + 512])
-
-        turned = {}
-
-        def turn(name, half, g, i):
-            b = bank()
-            turned[(name, half, g, i)] = b
-            bv = b[:].rearrange("p (u n) -> p u n", u=2)
-            for r in range(2):
-                words = rows_raw[(name, half)][:, 2 * i + r, :].bitcast(F32)
-                for u in range(2):
-                    nc.tensor.transpose(bv[:, u, 128 * r : 128 * r + 128], words[:, 256 * g + u : 256 * (g + 1) : 2], ident[:])
-
-        def turn_out(engine, name, half, g, i):
-            key = ("%s%d" % (name, half), g)
-            grp = grouped[key] if key in grouped else new_grouped(key)
-            copy_out(
-                engine,
-                grp[:, 1024 * i : 1024 * i + 1024].bitcast(F32).rearrange("p (n u) -> p n u", u=2),
-                turned[(name, half, g, i)][:].rearrange("p (u n) -> p n u", u=2),
+        def quantize(name, g):
+            new_codes((name, g))
+            nc.vector.quantize_mx(
+                out=codes[(name, g)][:].bitcast(FP8X4), scales=scales[(name, g)][:], in_=grouped[(name, g)][:]
             )
 
-        def mm(out_ap, lkey, lcols, rkey, start, stop):
+        def transpose_tokens(name, half, g, i):
+            banks[(name, half, g, i)] = new_bank()
+            out_tokens = banks[(name, half, g, i)][:].rearrange("p (u n) -> p u n", u=2)
+            for r in range(2):
+                words = raw[(name, half)][:, 2 * i + r, :].bitcast(F32)
+                for u in range(2):
+                    nc.tensor.transpose(
+                        out_tokens[:, u, 128 * r : 128 * r + 128], words[:, 256 * g + u : 256 * (g + 1) : 2], ident[:]
+                    )
+
+        def copy_tokens(engine, name, half, g, i):
+            key = ("%s%d" % (name, half), g)
+            words = grouped[key] if key in grouped else new_grouped(key)
+            copy(
+                engine,
+                words[:, 1024 * i : 1024 * i + 1024].bitcast(F32).rearrange("p (n u) -> p n u", u=2),
+                banks[(name, half, g, i)][:].rearrange("p (u n) -> p n u", u=2),
+            )
+
+        def matmul_pass(bank, left, columns, right, start, stop):
             nc.tensor.matmul_mx(
-                out=out_ap,
-                lhsT=codes[lkey][:, lcols].bitcast(FP8X4),
-                lhsT_scale=scales[lkey][:, lcols],
-                rhs=codes[rkey][:].bitcast(FP8X4),
-                rhs_scale=scales[rkey][:],
+                out=bank[:],
+                lhsT=codes[left][:, columns].bitcast(FP8X4),
+                lhsT_scale=scales[left][:, columns],
+                rhs=codes[right][:].bitcast(FP8X4),
+                rhs_scale=scales[right][:],
                 start=start,
                 stop=stop,
             )
 
-        psums = {}
+        def multiply(name, half, t):
+            terms = {"up": ("rh",), "prior": ("rp",), "mh": ("mh",), "diff": ("mh", "mp")}[name]
+            banks[(name, half, t)] = new_bank()
+            passes = [(term, g) for term in terms for g in range(2)]
+            for i in range(len(passes)):
+                term, g = passes[i]
+                tokens = "%s%d" % ("d" if term in ("mh", "rh") else "h", half)
+                matmul_pass(
+                    banks[(name, half, t)],
+                    (term, g),
+                    slice(128 * t, 128 * t + 128),
+                    (tokens, g),
+                    start=(i == 0),
+                    stop=(i == len(passes) - 1),
+                )
 
-        def channels(what, half, t):
-            dk, hk = "d%d" % half, "h%d" % half
-            terms = {"h": [("qr", dk)], "p": [("pr", hk)], "m": [("qm", dk)], "D": [("qm", dk), ("pm", hk)]}[what]
-            b = bank()
-            psums[(what, half, t)] = b
-            n = 2 * len(terms)
-            for i in range(n):
-                w, x = terms[i // 2]
-                mm(b[:], (w, i % 2), slice(128 * t, 128 * t + 128), (x, i % 2), i == 0, i == n - 1)
-
-        sg = {}
-        sp = {}
-
-        def sig(br, half, t):
-            if (br, half) not in sg:
-                sg[(br, half)] = big(F32, [P, 4, 512])
+        def sigmoid(branch, half, t):
+            if (branch, half) not in work_a:
+                work_a[(branch, half)] = new_slot([P, 4, HALF], F32)
             nc.scalar.activation(
-                out=sg[(br, half)][:, t, :], in_=psums[(br, half, t)][:], func=ACT.Sigmoid, scale=-1.0 if br == "h" else 1.0
+                out=work_a[(branch, half)][:, t, :],
+                in_=banks[(branch, half, t)][:],
+                func=ACT.Sigmoid,
+                scale=-1.0 if branch == "up" else 1.0,
             )
 
-        def ln(br, half, t):
-            l = sg[(br, half)][:, t, :]
-            if br == "h":
-                nc.scalar.activation(out=l, in_=l, func=ACT.Ln, bias=LN_FLOOR)
+        def log_sigmoid(branch, half, q):
+            x = work_a[(branch, half)][:, 2 * q : 2 * q + 2, :]
+            if branch == "up":
+                nc.scalar.activation(out=x, in_=x, func=ACT.Ln, bias=LN_FLOOR)
             else:
-                nc.scalar.activation(out=l, in_=l, func=ACT.Ln, bias=LN_FLOOR * SHIFT, scale=SHIFT)
+                nc.scalar.activation(out=x, in_=x, func=ACT.Ln, bias=LN_FLOOR * LN_SCALE, scale=LN_SCALE)
 
-        def softplus(br, half, t):
-            if (br, half) not in sp:
-                sp[(br, half)] = big(F32, [P, 4, 512])
-            l = sg[(br, half)][:, t, :]
-            o = sp[(br, half)][:, t, :]
-            s = psums[(br, half, t)]
-            if br == "h":
-                nc.vector.scalar_tensor_tensor(out=o, in0=l, scalar=-1.0, in1=s[:], op0=ALU.mult, op1=ALU.max)
+        def softplus(branch, half, t):
+            if (branch, half) not in work_b:
+                work_b[(branch, half)] = new_slot([P, 4, HALF], F32)
+            log_sig = work_a[(branch, half)][:, t, :]
+            result = work_b[(branch, half)][:, t, :]
+            s = banks[(branch, half, t)]
+            if branch == "up":
+                nc.vector.scalar_tensor_tensor(out=result, in0=log_sig, scalar=-1.0, in1=s[:], op0=ALU.mult, op1=ALU.max)
             else:
-                nc.vector.scalar_tensor_tensor(out=o, in0=s[:], scalar=VAR_MIN, in1=l, op0=ALU.subtract, op1=ALU.min)
+                nc.vector.scalar_tensor_tensor(out=result, in0=s[:], scalar=VAR_MIN, in1=log_sig, op0=ALU.subtract, op1=ALU.min)
 
-        def log_var(br, half, q):
-            ts = slice(2 * q, 2 * q + 2)
-            v = sp[(br, half)][:, ts, :]
-            o = v if br == "h" else sg[("p", half)][:, ts, :]
-            nc.scalar.activation(out=o, in_=v, func=ACT.Ln, bias=VAR_MIN if br == "h" else 0.0, scale=1.0 if br == "h" else -1.0)
-
-        def pick(engine):
-            return nc.gpsimd if engine == "G" else nc.vector
+        def log_variance(branch, half, q):
+            tiles = slice(2 * q, 2 * q + 2)
+            x = work_b[(branch, half)][:, tiles, :]
+            if branch == "up":
+                nc.scalar.activation(out=x, in_=x, func=ACT.Ln, bias=VAR_MIN, scale=1.0)
+            else:
+                nc.scalar.activation(out=work_a[("prior", half)][:, tiles, :], in_=x, func=ACT.Ln, bias=0.0, scale=-1.0)
 
         def log_ratio(engine, half, t):
-            vh = sp[("h", half)][:, t, :]
-            pick(engine).tensor_tensor(out=vh, in0=vh, in1=sg[("p", half)][:, t, :], op=ALU.subtract)
+            x = work_b[("up", half)][:, t, :]
+            vector_or_gpsimd(engine).tensor_tensor(out=x, in0=x, in1=work_a[("prior", half)][:, t, :], op=ALU.subtract)
 
         def weight(half, q):
-            w = sp[("h", half)][:, 2 * q : 2 * q + 2, :]
-            nc.scalar.activation(out=w, in_=w, func=ACT.Sigmoid)
+            x = work_b[("up", half)][:, 2 * q : 2 * q + 2, :]
+            nc.scalar.activation(out=x, in_=x, func=ACT.Sigmoid)
 
-        def merged_var(engine, half, t):
-            pick(engine).tensor_tensor(out=sg[("p", half)][:, t, :], in0=sp[("p", half)][:, t, :], in1=sp[("h", half)][:, t, :], op=ALU.mult)
+        def merged_variance(engine, half, t):
+            vector_or_gpsimd(engine).tensor_tensor(
+                out=work_a[("prior", half)][:, t, :],
+                in0=work_b[("prior", half)][:, t, :],
+                in1=work_b[("up", half)][:, t, :],
+                op=ALU.mult,
+            )
 
-        def root(half, q):
-            v = sg[("p", half)][:, 2 * q : 2 * q + 2, :]
-            nc.scalar.activation(out=v, in_=v, func=ACT.Sqrt, scale=-1.0)
+        def deviation(half, q):
+            x = work_a[("prior", half)][:, 2 * q : 2 * q + 2, :]
+            nc.scalar.activation(out=x, in_=x, func=ACT.Sqrt, scale=-1.0)
 
         def shift(half, t):
             nc.vector.scalar_tensor_tensor(
-                out=sg[("h", half)][:, t, :],
-                in0=sp[("h", half)][:, t, :],
+                out=work_a[("up", half)][:, t, :],
+                in0=work_b[("up", half)][:, t, :],
                 scalar=gain[:, t : t + 1],
-                in1=psums[("D", half, t)][:],
+                in1=banks[("diff", half, t)][:],
                 op0=ALU.mult,
                 op1=ALU.mult,
             )
 
         def mean(half, t):
-            x = sg[("h", half)][:, t, :]
+            x = work_a[("up", half)][:, t, :]
             nc.vector.scalar_tensor_tensor(
-                out=x, in0=psums[("m", half, t)][:], scalar=gain[:, t : t + 1], in1=x, op0=ALU.mult, op1=ALU.subtract
+                out=x, in0=banks[("mh", half, t)][:], scalar=gain[:, t : t + 1], in1=x, op0=ALU.mult, op1=ALU.subtract
             )
 
-        def turn_eps(half, u):
-            b = bank()
-            psums[("eps", half, u)] = b
+        def transpose_eps(half, u):
+            banks[("eps", half, u)] = new_bank()
             for r in range(4):
-                words = misc_raw[half][:, r, :].bitcast(F32)
-                nc.tensor.transpose(b[:, 128 * r : 128 * r + 128], words[:, u:256:2], ident[:])
+                words = raw[("eps", half)][:, r, :].bitcast(F32)
+                nc.tensor.transpose(banks[("eps", half, u)][:, 128 * r : 128 * r + 128], words[:, u:256:2], ident[:])
 
         def sample(half, t):
-            ev = psums[("eps", half, t // 2)][:].bitcast(BF16).rearrange("p (n e) -> p n e", e=2)[:, :, t % 2]
+            pairs = banks[("eps", half, t // 2)][:].bitcast(BF16).rearrange("p (n e) -> p n e", e=2)
             nc.vector.scalar_tensor_tensor(
-                out=sp[("p", half)][:, t, :], in0=sg[("p", half)][:, t, :], scalar=gain[:, t : t + 1], in1=ev, op0=ALU.mult, op1=ALU.mult
+                out=work_b[("prior", half)][:, t, :],
+                in0=work_a[("prior", half)][:, t, :],
+                scalar=gain[:, t : t + 1],
+                in1=pairs[:, :, t % 2],
+                op0=ALU.mult,
+                op1=ALU.mult,
             )
 
-        def latent(engine, half, i):
+        def latent(engine, half, r):
             key = ("z%d" % half, 0)
-            grp = grouped[key] if key in grouped else new_grouped(key)
-            n = slice(256 * i, 256 * i + 256)
-            (nc.gpsimd if engine == "G" else nc.vector).tensor_tensor(
-                out=grp[:, 1024 * i : 1024 * i + 1024].rearrange("p (n k t) -> p n t k", k=4, t=4),
-                in0=sg[("h", half)][:, :, n].rearrange("p t (n k) -> p n t k", k=4),
-                in1=sp[("p", half)][:, :, n].rearrange("p t (n k) -> p n t k", k=4),
-                op=ALU.add,
-            )
+            words = grouped[key] if key in grouped else new_grouped(key)
+            tokens = slice(128 * r, 128 * r + 128)
+            z = words[:, 512 * r : 512 * r + 512]
+            mean_part = work_a[("up", half)][:, :, tokens]
+            noise_part = work_b[("prior", half)][:, :, tokens]
+            if engine == "G":
+                nc.gpsimd.tensor_tensor(
+                    out=z.rearrange("p (n t) -> p n t", t=4),
+                    in0=mean_part.rearrange("p t n -> p n t"),
+                    in1=noise_part.rearrange("p t n -> p n t"),
+                    op=ALU.add,
+                )
+            else:
+                nc.vector.tensor_tensor(
+                    out=z.rearrange("p (n i t) -> p n t i", i=4, t=4),
+                    in0=mean_part.rearrange("p t (n i) -> p n t i", i=4),
+                    in1=noise_part.rearrange("p t (n i) -> p n t i", i=4),
+                    op=ALU.add,
+                )
 
-        def quant_z(half, i):
+        def quantize_latent(half, i):
             key = ("z%d" % half, 0)
             if key not in codes:
-                codes[key] = keep.tile([P, 512], U32, name="codes_%s_%d" % key, align_bytes=64)
-                scales[key] = keep.tile([P, 512], U8, name="scales_%s_%d" % key, align_bytes=64)
-            n = slice(256 * i, 256 * i + 256)
+                new_codes(key)
+            tokens = slice(256 * i, 256 * i + 256)
             nc.vector.quantize_mx(
-                out=codes[key][:, n].bitcast(FP8X4), scales=scales[key][:, n], in_=grouped[key][:, 1024 * i : 1024 * i + 1024]
+                out=codes[key][:, tokens].bitcast(FP8X4),
+                scales=scales[key][:, tokens],
+                in_=grouped[key][:, 1024 * i : 1024 * i + 1024],
             )
 
-        def project_x(half, r, c):
-            b = bank()
-            psums[("o", half, r, c)] = b
+        def project_tokens(half, r, c):
+            banks[("out", half, r, c)] = new_bank()
             for g in range(2):
-                mm(b[:], ("h%d" % half, g), slice(128 * r, 128 * r + 128), ("x%d" % c, g), g == 0, False)
+                matmul_pass(
+                    banks[("out", half, r, c)],
+                    ("h%d" % half, g),
+                    slice(128 * r, 128 * r + 128),
+                    ("px%d" % c, g),
+                    start=(g == 0),
+                    stop=False,
+                )
 
-        def project_z(half, r, c):
-            mm(psums[("o", half, r, c)][:], ("z%d" % half, 0), slice(128 * r, 128 * r + 128), ("w%d" % c, 0), False, True)
-
-        o_tiles = {}
+        def project_latent(half, r, c):
+            matmul_pass(
+                banks[("out", half, r, c)],
+                ("z%d" % half, 0),
+                slice(128 * r, 128 * r + 128),
+                ("wz%d" % c, 0),
+                start=False,
+                stop=True,
+            )
 
         def finish(engine, half, r, c):
-            if (half, r) not in o_tiles:
-                o_tiles[(half, r)] = big(F32, [P, 1024])
-            copy_out(engine, o_tiles[(half, r)][:, 512 * c : 512 * c + 512], psums[("o", half, r, c)][:])
+            if (half, r) not in rows_out:
+                rows_out[(half, r)] = new_slot([P, 1024], F32)
+            copy(engine, rows_out[(half, r)][:, 512 * c : 512 * c + 512], banks[("out", half, r, c)][:])
 
         def store(half, r, c):
-            n = slice(512 * c, 512 * c + 512)
+            columns = slice(512 * c, 512 * c + 512)
             nc.sync.dma_start(
-                out=out[HALF * half : HALF * half + HALF, n].rearrange("(p r) n -> p r n", r=4)[:, r, :], in_=o_tiles[(half, r)][:, n]
+                out=out[HALF * half : HALF * half + HALF, columns].rearrange("(p r) n -> p r n", r=4)[:, r, :],
+                in_=rows_out[(half, r)][:, columns],
             )
 
-        def load_bytes(g):
-            if g == 0:
-                load_wp(0, 0, 1)
-                load_wp(0, 1, 2)
-            else:
-                load_wp(1, 0, 2)
-            load_wp(g, 2, 4)
-
-        def load_tokens(name, half):
-            for i in range(2):
-                load_rows(name, half, i)
-
-        def quant_rows(name):
-            for g in range(2):
-                quant(name, g)
-
-        def turn2(name, half, g):
-            for i in range(2):
-                turn(name, half, g, i)
-
-        def turn_out2(engine, name, half, g):
-            for i in range(2):
-                turn_out(engine, name, half, g, i)
-
-        def channels2(what, half, q):
-            for t in (2 * q, 2 * q + 1):
-                channels(what, half, t)
-
-        def sig2(br, half, q):
-            for t in (2 * q, 2 * q + 1):
-                sig(br, half, t)
-
-        def ln2(br, half, q):
-            for t in (2 * q, 2 * q + 1):
-                ln(br, half, t)
-
-        def softplus2(br, half, q):
-            for t in (2 * q, 2 * q + 1):
-                softplus(br, half, t)
-
-        def shift2(half, q):
-            for t in (2 * q, 2 * q + 1):
-                shift(half, t)
-
-        def mean2(half, q):
-            for t in (2 * q, 2 * q + 1):
-                mean(half, t)
-
-        def sample2(half, q):
-            for t in (2 * q, 2 * q + 1):
-                sample(half, t)
-
-        def project_x2(half, r):
-            for c in range(2):
-                project_x(half, r, c)
-
-        def project_z2(half, r):
-            for c in range(2):
-                project_z(half, r, c)
-
         load_scale()
-        negate_scale()
         load_bytes(0)
-        load_tokens("h", 1)
-        widen("V", 0, 1, 0)
-        load_bytes(1)
-        group_p("V", 1, 0)
-        turn2("h", 1, 1)
-        widen("V", 1, 1, 0)
-        widen("S", 0, 0, 0)
-        quant("pr", 0)
-        widen("V", 0, 1, 1)
-        group_p("S", 0, 0)
-        turn2("h", 1, 0)
-        load_tokens("d", 1)
-        turn_out2("S", "h", 1, 1)
-        load_wq(0)
-        quant("pm", 0)
-        turn2("d", 1, 1)
         load_tokens("h", 0)
-        widen("S", 1, 1, 1)
-        widen("V", 0, 0, 1)
-        turn_out2("S", "h", 1, 0)
-        group_p("V", 1, 1)
-        widen("V", 1, 0, 1)
-        quant("pr", 1)
-        turn2("d", 1, 0)
-        quant_rows("h1")
-        channels2("p", 1, 0)
-        turn_out2("S", "d", 1, 1)
-        turn_out2("S", "d", 1, 0)
-        turn2("h", 0, 0)
-        group_q("V", 1, 0)
-        quant_rows("d1")
+        load_bytes(1)
         load_tokens("d", 0)
-        turn2("h", 0, 1)
-        group_q("V", 0, 0)
-        sig2("p", 1, 0)
-        turn2("d", 0, 1)
-        load_wq(1)
-        turn_out2("S", "h", 0, 0)
+        for g in range(2):
+            load_wq(g)
+        for name in ("d", "h"):
+            load_tokens(name, 1)
         load_wz()
-        turn_out2("S", "h", 0, 1)
-        turn_out2("S", "d", 0, 1)
-        quant_rows("h0")
-        group_q("V", 1, 1)
-        channels2("p", 1, 1)
-        turn2("d", 0, 0)
-        sig2("p", 1, 1)
-        quant("qr", 0)
-        channels2("p", 0, 1)
-        turn_out2("S", "d", 0, 0)
-        quant("qr", 1)
-        channels2("h", 1, 0)
-        group_w("V", 0)
-        group_x("V", 1, 1)
-        quant("qm", 0)
-        sig2("p", 0, 1)
-        sig2("h", 1, 0)
-        widen("V", 1, 0, 0)
-        ln2("h", 1, 0)
-        load_eps(1)
-        group_q("V", 0, 1)
-        quant_rows("d0")
-        softplus2("h", 1, 0)
-        ln2("p", 1, 0)
-        channels2("p", 0, 0)
-        ln2("p", 0, 1)
-        softplus2("p", 1, 0)
-        group_x("V", 1, 0)
-        channels2("h", 0, 0)
-        ln2("p", 1, 1)
-        log_var("h", 1, 0)
-        softplus2("p", 0, 1)
         load_gain()
-        channels2("h", 1, 1)
-        softplus2("p", 1, 1)
-        quant("x1", 0)
-        log_var("p", 1, 0)
-        channels2("h", 0, 1)
-        log_ratio("G", 1, 0)
-        sig2("h", 1, 1)
-        sig2("h", 0, 1)
-        sig2("p", 0, 0)
-        log_ratio("V", 1, 1)
-        group_p("V", 0, 1)
-        group_x("V", 0, 1)
-        quant("qm", 1)
-        quant("x1", 1)
-        sig2("h", 0, 0)
-        group_w("V", 1)
-        weight(1, 0)
-        ln2("h", 0, 0)
-        ln2("h", 1, 1)
-        group_x("V", 0, 0)
-        softplus2("h", 0, 0)
-        quant("w0", 0)
-        log_var("h", 0, 0)
-        quant("pm", 1)
-        log_var("p", 1, 1)
-        softplus2("h", 1, 1)
-        channels2("D", 1, 0)
-        merged_var("G", 1, 1)
-        ln2("p", 0, 0)
-        ln2("h", 0, 1)
-        quant("w1", 0)
-        channels2("D", 1, 1)
-        softplus2("p", 0, 0)
+        for half in range(2):
+            load_eps(half)
+
+        negate_scale()
+        for g in range(2):
+            for i in range(2):
+                transpose_tokens("h", 0, g, i)
+        for engine, name in (("S", "rp"), ("V", "px0")):
+            widen(engine, name, 0)
+        lay_out("S", "px0", 0)
+        widen("V", "mp", 0)
+        for name in ("rp", "mp"):
+            lay_out("V", name, 0)
+        for engine, name in (("V", "rp"), ("S", "px1")):
+            widen(engine, name, 1)
+        for g in range(2):
+            for i in range(2):
+                copy_tokens("S", "h", 0, g, i)
+        for g in range(2):
+            for i in range(2):
+                transpose_tokens("d", 0, g, i)
+        for name in ("rp", "px0"):
+            quantize(name, 0)
+        lay_out("V", "rp", 1)
+        copy_tokens("S", "d", 0, 0, 0)
+        widen("S", "mp", 1)
+        for g in range(2):
+            quantize("h0", g)
+        quantize("mp", 0)
+        quantize("rp", 1)
+        for g, i in ((0, 1), (1, 0), (1, 1)):
+            copy_tokens("S", "d", 0, g, i)
+        for t in range(4):
+            multiply("prior", 0, t)
+        for t in range(2):
+            sigmoid("prior", 0, t)
+        for g in range(2):
+            lay_out("V", "rh", g)
+        for g in range(2):
+            for i in range(2):
+                transpose_tokens("d", 1, g, i)
+        for t in range(2, 4):
+            sigmoid("prior", 0, t)
+        for name in ("d0", "rh"):
+            for g in range(2):
+                quantize(name, g)
+        for engine, g, i in (("S", 0, 0), ("V", 0, 1), ("S", 1, 0), ("S", 1, 1)):
+            copy_tokens(engine, "d", 1, g, i)
+        for t in range(4):
+            multiply("up", 0, t)
+        widen("V", "px1", 0)
+        for t in range(4):
+            sigmoid("up", 0, t)
+        for name in ("px1", "mp"):
+            lay_out("V", name, 1)
+        for g in range(2):
+            quantize("d1", g)
+
+        for branch, q in (("up", 1), ("prior", 0), ("prior", 1)):
+            log_sigmoid(branch, 0, q)
+        lay_out("V", "mh", 0)
+        for branch, t in (("up", 2), ("up", 3), ("prior", 0), ("prior", 1), ("prior", 2), ("prior", 3)):
+            softplus(branch, 0, t)
+        widen("V", "px0", 1)
+        for g in range(2):
+            for i in range(2):
+                transpose_tokens("h", 1, g, i)
+        log_sigmoid("up", 0, 0)
+        for branch, q in (("up", 1), ("prior", 1), ("prior", 0)):
+            log_variance(branch, 0, q)
+        for t in range(2):
+            softplus("up", 0, t)
+        for engine, g, i in (("V", 0, 0), ("S", 0, 1), ("V", 1, 0), ("V", 1, 1)):
+            copy_tokens(engine, "h", 1, g, i)
+        for name, g in (("h1", 0), ("h1", 1), ("mh", 0)):
+            quantize(name, g)
+        log_variance("up", 0, 0)
+        for name in ("up", "prior"):
+            for t in range(4):
+                multiply(name, 1, t)
+        for engine, t in (("V", 0), ("V", 1), ("G", 2), ("G", 3)):
+            log_ratio(engine, 0, t)
+        for name in ("wz0", "wz1"):
+            lay_out("V", name, 0)
+        for branch in ("up", "prior"):
+            for t in range(4):
+                sigmoid(branch, 1, t)
+        lay_out("V", "mh", 1)
+        for q in range(2):
+            weight(0, q)
+
+        log_sigmoid("up", 1, 0)
+        for name in ("mp", "mh", "px1"):
+            quantize(name, 1)
+        for name, g in (("px0", 1), ("px1", 0)):
+            lay_out("V", name, g)
+        for branch, q in (("up", 1), ("prior", 0), ("prior", 1)):
+            log_sigmoid(branch, 1, q)
+        for branch in ("up", "prior"):
+            for t in range(4):
+                softplus(branch, 1, t)
+
         widen_gain()
-        quant("x0", 0)
-        merged_var("V", 1, 0)
-        softplus2("h", 0, 1)
-        channels2("m", 1, 0)
-        log_var("h", 1, 1)
-        quant("x0", 1)
-        log_var("p", 0, 1)
-        log_var("p", 0, 0)
-        shift2(1, 0)
-        log_var("h", 0, 1)
-        log_ratio("G", 1, 3)
-        channels2("D", 0, 1)
-        log_ratio("V", 1, 2)
-        turn_eps(1, 1)
-        log_ratio("V", 0, 3)
-        log_ratio("G", 0, 2)
-        mean2(1, 0)
-        weight(1, 1)
-        log_ratio("G", 0, 1)
-        shift2(1, 1)
-        log_ratio("G", 0, 0)
-        weight(0, 1)
-        shift2(0, 1)
-        merged_var("G", 1, 2)
-        weight(0, 0)
-        merged_var("G", 1, 3)
-        channels2("m", 0, 1)
-        mean2(0, 1)
-        root(1, 0)
-        channels2("D", 0, 0)
-        merged_var("G", 0, 0)
-        turn_eps(1, 0)
-        channels2("m", 1, 1)
-        shift2(0, 0)
-        mean2(1, 1)
-        merged_var("G", 0, 1)
-        merged_var("G", 0, 2)
-        channels2("m", 0, 0)
-        sample2(1, 0)
-        root(1, 1)
-        load_eps(0)
-        project_x2(1, 2)
-        sample2(1, 1)
-        mean2(0, 0)
-        root(0, 0)
-        merged_var("G", 0, 3)
-        root(0, 1)
-        project_x2(1, 3)
-        turn_eps(0, 1)
-        turn_eps(0, 0)
-        latent("V", 1, 1)
-        project_x2(1, 0)
-        quant_z(1, 1)
-        project_z2(1, 3)
-        latent("V", 1, 0)
-        project_z2(1, 2)
-        finish("S", 1, 3, 0)
-        finish("S", 1, 2, 0)
-        quant_z(1, 0)
-        project_x2(1, 1)
-        project_z2(1, 0)
-        project_z2(1, 1)
-        finish("S", 1, 3, 1)
-        sample2(0, 1)
-        project_x2(0, 0)
-        store(1, 2, 0)
-        sample2(0, 0)
-        latent("V", 0, 0)
-        finish("S", 1, 2, 1)
-        project_x2(0, 1)
-        store(1, 3, 1)
-        store(1, 3, 0)
-        finish("S", 1, 0, 0)
-        finish("S", 1, 1, 1)
-        finish("S", 1, 1, 0)
-        quant_z(0, 0)
-        project_z2(0, 1)
-        latent("V", 0, 1)
-        finish("V", 0, 1, 1)
-        finish("S", 1, 0, 1)
-        project_z2(0, 0)
-        quant_z(0, 1)
-        store(1, 0, 0)
-        finish("V", 0, 0, 1)
-        store(1, 1, 1)
-        store(1, 2, 1)
-        finish("S", 0, 1, 0)
-        store(1, 1, 0)
-        store(1, 0, 1)
-        store(0, 1, 0)
-        store(0, 1, 1)
-        finish("V", 0, 0, 0)
-        project_x2(0, 2)
-        project_z2(0, 2)
-        finish("V", 0, 2, 1)
-        store(0, 0, 1)
-        finish("V", 0, 2, 0)
-        store(0, 0, 0)
-        project_x2(0, 3)
-        project_z2(0, 3)
-        finish("V", 0, 3, 0)
-        store(0, 2, 1)
-        store(0, 2, 0)
-        store(0, 3, 0)
-        finish("V", 0, 3, 1)
-        store(0, 3, 1)
+        for name in ("diff", "mh"):
+            for t in range(4):
+                multiply(name, 0, t)
+        for name, g in (("wz0", 0), ("px0", 1), ("px1", 0)):
+            quantize(name, g)
+        for t in range(4):
+            shift(0, t)
+        for t in range(2):
+            mean(0, t)
+        for t in range(4):
+            merged_variance("G", 0, t)
+        for half in range(2):
+            for u in range(2):
+                transpose_eps(half, u)
+        for branch in ("up", "prior"):
+            for q in range(2):
+                log_variance(branch, 1, q)
+        for q in range(2):
+            deviation(0, q)
+        for t in range(2, 4):
+            mean(0, t)
+        for name, t in (("diff", 0), ("diff", 1), ("diff", 2), ("mh", 0)):
+            multiply(name, 1, t)
+        for t in range(4):
+            log_ratio("G", 1, t)
+        for t in range(4):
+            sample(0, t)
+        quantize("wz1", 0)
+        for name, t in (("diff", 3), ("mh", 1)):
+            multiply(name, 1, t)
+        for r in range(2):
+            latent("V", 0, r)
+        for q in range(2):
+            weight(1, q)
+        for engine, t in (("V", 0), ("G", 1), ("G", 2)):
+            merged_variance(engine, 1, t)
+        for t in range(4):
+            shift(1, t)
+        quantize_latent(0, 0)
+        for t in range(2, 4):
+            multiply("mh", 1, t)
+        merged_variance("G", 1, 3)
+
+        for r in range(2):
+            project_tokens(0, r, 1)
+        for r in range(2):
+            project_latent(0, r, 1)
+        for t in range(4):
+            mean(1, t)
+        for q in range(2):
+            deviation(1, q)
+        for r in range(2):
+            project_tokens(0, r, 0)
+        for r in (2, 3):
+            latent("G", 0, r)
+        for t in range(4):
+            sample(1, t)
+        for r in range(2):
+            project_latent(0, r, 0)
+        for r in (2, 3):
+            for c in range(2):
+                project_tokens(0, r, c)
+        quantize_latent(0, 1)
+        for r in range(2):
+            latent("V", 1, r)
+        quantize_latent(1, 0)
+        for r in (2, 3):
+            latent("V", 1, r)
+        for r in range(2):
+            for c in range(2):
+                finish("S", 0, r, c)
+        for r in (2, 3):
+            for c in range(2):
+                project_latent(0, r, c)
+        quantize_latent(1, 1)
+        for r in (2, 3):
+            for c in range(2):
+                finish("S", 0, r, c)
+        for r in range(4):
+            for c in range(2):
+                store(0, r, c)
+
+        for r in range(4):
+            for c in range(2):
+                project_tokens(1, r, c)
+                project_latent(1, r, c)
+                finish("V", 1, r, c)
+                store(1, r, c)

import math
from contextlib import ExitStack

import concourse.mybir as mybir
from concourse.masks import make_identity

P = 128
HALF = 512
PASS = 512
F32 = mybir.dt.float32
BF16 = mybir.dt.bfloat16
U32 = mybir.dt.uint32
U8 = mybir.dt.uint8
F8 = mybir.dt.float8_e4m3fn
FP8X4 = mybir.dt.float8_e4m3fn_x4
ACT = mybir.ActivationFunctionType
ALU = mybir.AluOpType

FLOPS = 2 * 1024 * 1024 * 3072 + 2 * 1024 * 512 * 1024
VAR_MIN = 0.05
LN_FLOOR = 2.0**-60
LN_SCALE = math.exp(-VAR_MIN)
FIRST_COLUMN = {"mp": 0, "rp": 512, "px0": 1024, "px1": 1536, "mh": 0, "rh": 512, "wz0": 0, "wz1": 512}


def tile_laddertopdownprecisionmerge_kernel(tc, h, d, eps, wp_bytes, wp_scale, wq, gz, wz, out):
    nc = tc.nc
    with ExitStack() as ctx:
        keep = ctx.enter_context(tc.tile_pool(name="keep", bufs=1))
        work = ctx.enter_context(tc.tile_pool(name="work", bufs=1))
        psum = ctx.enter_context(tc.psum_pool(name="psum", bufs=8))
        ctx.enter_context(tc.manual_schedule())

        first = keep.tile([P, 1], F32)
        nc.vector.memset(first[:], 0.0)
        nc.scalar.activation(out=first[:], in_=first[:], func=ACT.Sigmoid)
        ident = keep.tile([P, P], F32)
        make_identity(nc, ident[:])

        scale = keep.tile([P, 8], F32)
        neg_scale = keep.tile([P, 8], F32)
        gain_bf16 = keep.tile([P, 4], BF16)
        gain = keep.tile([P, 4], F32)

        raw = {}
        wp_codes = {}
        wide = {}
        grouped = {}
        codes = {}
        scales = {}
        banks = {}
        work_a = {}
        work_b = {}
        rows_out = {}

        def new_slot(shape, dtype):
            tile = work.tile(shape, dtype, tag="slot", name="slot", bufs=15, align_bytes=64)
            return tile

        def new_grouped(key):
            tile = work.tile([P, 4 * PASS], BF16, tag="grouped", name="grouped", bufs=5, align_bytes=64)
            grouped[key] = tile
            return tile

        def new_bank():
            tile = psum.tile([P, 512], F32, tag="bank", name="bank")
            return tile

        def new_codes(key):
            codes[key] = keep.tile([P, PASS], U32, name="codes_%s_%d" % key, align_bytes=64)
            scales[key] = keep.tile([P, PASS], U8, name="scales_%s_%d" % key, align_bytes=64)

        def copy(engine, out_ap, in_ap):
            if engine == "S":
                nc.scalar.copy(out=out_ap, in_=in_ap)
            else:
                nc.vector.tensor_copy(out=out_ap, in_=in_ap)

        def vector_or_gpsimd(engine):
            return nc.gpsimd if engine == "G" else nc.vector
        def load_scale():
            nc.sync.dma_start(
                out=scale[:].rearrange("p (g j) -> p g j", g=2), in_=wp_scale.rearrange("(g p j) o -> p g (j o)", p=P, j=4)
            )

        def load_gain():
            nc.sync.dma_start(out=gain_bf16[:], in_=gz.rearrange("(p t) -> p t", t=4))

        def load_bytes(g):
            wp_codes[g] = keep.tile([P, 4, 2048], U8, name="wp_codes_%d" % g, align_bytes=64)
            rows = wp_bytes[PASS * g : PASS * g + PASS, :].rearrange("(p j) n -> p j n", j=4)
            for j0, j1 in ((0, 1), (1, 2), (2, 4)) if g == 0 else ((0, 2), (2, 4)):
                nc.sync.dma_start(out=wp_codes[g][:, j0:j1, :], in_=rows[:, j0:j1, :])

        def load_tokens(name, half):
            raw[(name, half)] = new_slot([P, 4, 1024], BF16)
            rows = (d if name == "d" else h)[HALF * half : HALF * half + HALF, :].rearrange("(p r) k -> p r k", r=4)
            for i in range(2):
                nc.sync.dma_start(out=raw[(name, half)][:, 2 * i : 2 * i + 2, :], in_=rows[:, 2 * i : 2 * i + 2, :])

        def load_wq(g):
            raw[("wq", g)] = new_slot([P, 4, 1024], BF16)
            nc.sync.dma_start(out=raw[("wq", g)][:], in_=wq[PASS * g : PASS * g + PASS, :].rearrange("(p j) n -> p j n", j=4))

        def load_wz():
            raw["wz"] = new_slot([P, 4, 1024], BF16)
            nc.sync.dma_start(out=raw["wz"][:], in_=wz.rearrange("(p j) n -> p j n", j=4))

        def load_eps(half):
            raw[("eps", half)] = new_slot([P, 4, 512], BF16)
            nc.sync.dma_start(
                out=raw[("eps", half)][:], in_=eps[HALF * half : HALF * half + HALF, :].rearrange("(p r) c -> p r c", r=4)
            )

        def negate_scale():
            nc.vector.tensor_scalar(out=neg_scale[:], in0=scale[:], scalar1=-1.0, scalar2=None, op0=ALU.mult)

        def widen_gain():
            nc.vector.tensor_copy(out=gain[:], in_=gain_bf16[:])

        def widen(engine, name, g):
            wide[(name, g)] = work.tile([P, 4, 512], BF16, tag="wide", name="wide", bufs=4, align_bytes=64)
            factors = neg_scale if name in ("mp", "rp") else scale
            first = FIRST_COLUMN[name]
            for j in range(4):
                values = wp_codes[g][:, j, first : first + 512].bitcast(F8)
                factor = factors[:, 4 * g + j : 4 * g + j + 1]
                if engine == "S":
                    nc.scalar.activation(out=wide[(name, g)][:, j, :], in_=values, func=ACT.Copy, scale=factor)
                else:
                    nc.vector.tensor_scalar(out=wide[(name, g)][:, j, :], in0=values, scalar1=factor, scalar2=None, op0=ALU.mult)

        def lay_out(engine, name, g):
            if name in ("mh", "rh"):
                rows = raw[("wq", g)][:, :, FIRST_COLUMN[name] : FIRST_COLUMN[name] + 512]
            elif name in ("wz0", "wz1"):
                rows = raw["wz"][:, :, FIRST_COLUMN[name] : FIRST_COLUMN[name] + 512]
            else:
                rows = wide[(name, g)][:]
            words = new_grouped((name, g))
            if name in ("mp", "rp", "mh", "rh"):
                copy(engine, words[:].rearrange("p (t m j) -> p m j t", t=4, j=4), rows.rearrange("p j (m t) -> p m j t", t=4))
            else:
                copy(engine, words[:].rearrange("p (n i j) -> p n j i", i=4, j=4), rows.rearrange("p j (n i) -> p n j i", i=4))

        def quantize(name, g):
            new_codes((name, g))
            nc.vector.quantize_mx(
                out=codes[(name, g)][:].bitcast(FP8X4), scales=scales[(name, g)][:], in_=grouped[(name, g)][:]
            )

        def transpose_tokens(name, half, g, i):
            banks[(name, half, g, i)] = new_bank()
            out_tokens = banks[(name, half, g, i)][:].rearrange("p (u n) -> p u n", u=2)
            for r in range(2):
                words = raw[(name, half)][:, 2 * i + r, :].bitcast(F32)
                for u in range(2):
                    nc.tensor.transpose(
                        out_tokens[:, u, 128 * r : 128 * r + 128], words[:, 256 * g + u : 256 * (g + 1) : 2], ident[:]
                    )

        def copy_tokens(engine, name, half, g, i):
            key = ("%s%d" % (name, half), g)
            words = grouped[key] if key in grouped else new_grouped(key)
            copy(
                engine,
                words[:, 1024 * i : 1024 * i + 1024].bitcast(F32).rearrange("p (n u) -> p n u", u=2),
                banks[(name, half, g, i)][:].rearrange("p (u n) -> p n u", u=2),
            )

        def matmul_pass(bank, left, columns, right, start, stop):
            nc.tensor.matmul_mx(
                out=bank[:],
                lhsT=codes[left][:, columns].bitcast(FP8X4),
                lhsT_scale=scales[left][:, columns],
                rhs=codes[right][:].bitcast(FP8X4),
                rhs_scale=scales[right][:],
                start=start,
                stop=stop,
            )

        def multiply(name, half, t):
            terms = {"up": ("rh",), "prior": ("rp",), "mh": ("mh",), "diff": ("mh", "mp")}[name]
            banks[(name, half, t)] = new_bank()
            passes = [(term, g) for term in terms for g in range(2)]
            for i in range(len(passes)):
                term, g = passes[i]
                tokens = "%s%d" % ("d" if term in ("mh", "rh") else "h", half)
                matmul_pass(
                    banks[(name, half, t)],
                    (term, g),
                    slice(128 * t, 128 * t + 128),
                    (tokens, g),
                    start=(i == 0),
                    stop=(i == len(passes) - 1),
                )

        def sigmoid(branch, half, t):
            if (branch, half) not in work_a:
                work_a[(branch, half)] = new_slot([P, 4, HALF], F32)
            nc.scalar.activation(
                out=work_a[(branch, half)][:, t, :],
                in_=banks[(branch, half, t)][:],
                func=ACT.Sigmoid,
                scale=-1.0 if branch == "up" else 1.0,
            )

        def log_sigmoid(branch, half, q):
            x = work_a[(branch, half)][:, 2 * q : 2 * q + 2, :]
            if branch == "up":
                nc.scalar.activation(out=x, in_=x, func=ACT.Ln, bias=LN_FLOOR)
            else:
                nc.scalar.activation(out=x, in_=x, func=ACT.Ln, bias=LN_FLOOR * LN_SCALE, scale=LN_SCALE)

        def softplus(branch, half, t):
            if (branch, half) not in work_b:
                work_b[(branch, half)] = new_slot([P, 4, HALF], F32)
            log_sig = work_a[(branch, half)][:, t, :]
            result = work_b[(branch, half)][:, t, :]
            s = banks[(branch, half, t)]
            if branch == "up":
                nc.vector.scalar_tensor_tensor(out=result, in0=log_sig, scalar=-1.0, in1=s[:], op0=ALU.mult, op1=ALU.max)
            else:
                nc.vector.scalar_tensor_tensor(out=result, in0=s[:], scalar=VAR_MIN, in1=log_sig, op0=ALU.subtract, op1=ALU.min)

        def log_variance(branch, half, q):
            tiles = slice(2 * q, 2 * q + 2)
            x = work_b[(branch, half)][:, tiles, :]
            if branch == "up":
                nc.scalar.activation(out=x, in_=x, func=ACT.Ln, bias=VAR_MIN, scale=1.0)
            else:
                nc.scalar.activation(out=work_a[("prior", half)][:, tiles, :], in_=x, func=ACT.Ln, bias=0.0, scale=-1.0)

        def log_ratio(engine, half, t):
            x = work_b[("up", half)][:, t, :]
            vector_or_gpsimd(engine).tensor_tensor(out=x, in0=x, in1=work_a[("prior", half)][:, t, :], op=ALU.subtract)

        def weight(half, q):
            x = work_b[("up", half)][:, 2 * q : 2 * q + 2, :]
            nc.scalar.activation(out=x, in_=x, func=ACT.Sigmoid)

        def merged_variance(engine, half, t):
            vector_or_gpsimd(engine).tensor_tensor(
                out=work_a[("prior", half)][:, t, :],
                in0=work_b[("prior", half)][:, t, :],
                in1=work_b[("up", half)][:, t, :],
                op=ALU.mult,
            )

        def deviation(half, q):
            x = work_a[("prior", half)][:, 2 * q : 2 * q + 2, :]
            nc.scalar.activation(out=x, in_=x, func=ACT.Sqrt, scale=-1.0)

        def shift(half, t):
            nc.vector.scalar_tensor_tensor(
                out=work_a[("up", half)][:, t, :],
                in0=work_b[("up", half)][:, t, :],
                scalar=gain[:, t : t + 1],
                in1=banks[("diff", half, t)][:],
                op0=ALU.mult,
                op1=ALU.mult,
            )

        def mean(half, t):
            x = work_a[("up", half)][:, t, :]
            nc.vector.scalar_tensor_tensor(
                out=x, in0=banks[("mh", half, t)][:], scalar=gain[:, t : t + 1], in1=x, op0=ALU.mult, op1=ALU.subtract
            )

        def transpose_eps(half, u):
            banks[("eps", half, u)] = new_bank()
            for r in range(4):
                words = raw[("eps", half)][:, r, :].bitcast(F32)
                nc.tensor.transpose(banks[("eps", half, u)][:, 128 * r : 128 * r + 128], words[:, u:256:2], ident[:])

        def sample(half, t):
            pairs = banks[("eps", half, t // 2)][:].bitcast(BF16).rearrange("p (n e) -> p n e", e=2)
            nc.vector.scalar_tensor_tensor(
                out=work_b[("prior", half)][:, t, :],
                in0=work_a[("prior", half)][:, t, :],
                scalar=gain[:, t : t + 1],
                in1=pairs[:, :, t % 2],
                op0=ALU.mult,
                op1=ALU.mult,
            )

        def latent(engine, half, r):
            key = ("z%d" % half, 0)
            words = grouped[key] if key in grouped else new_grouped(key)
            tokens = slice(128 * r, 128 * r + 128)
            z = words[:, 512 * r : 512 * r + 512]
            mean_part = work_a[("up", half)][:, :, tokens]
            noise_part = work_b[("prior", half)][:, :, tokens]
            if engine == "G":
                nc.gpsimd.tensor_tensor(
                    out=z.rearrange("p (n t) -> p n t", t=4),
                    in0=mean_part.rearrange("p t n -> p n t"),
                    in1=noise_part.rearrange("p t n -> p n t"),
                    op=ALU.add,
                )
            else:
                nc.vector.tensor_tensor(
                    out=z.rearrange("p (n i t) -> p n t i", i=4, t=4),
                    in0=mean_part.rearrange("p t (n i) -> p n t i", i=4),
                    in1=noise_part.rearrange("p t (n i) -> p n t i", i=4),
                    op=ALU.add,
                )

        def quantize_latent(half, i):
            key = ("z%d" % half, 0)
            if key not in codes:
                new_codes(key)
            tokens = slice(256 * i, 256 * i + 256)
            nc.vector.quantize_mx(
                out=codes[key][:, tokens].bitcast(FP8X4),
                scales=scales[key][:, tokens],
                in_=grouped[key][:, 1024 * i : 1024 * i + 1024],
            )

        def project_tokens(half, r, c):
            banks[("out", half, r, c)] = new_bank()
            for g in range(2):
                matmul_pass(
                    banks[("out", half, r, c)],
                    ("h%d" % half, g),
                    slice(128 * r, 128 * r + 128),
                    ("px%d" % c, g),
                    start=(g == 0),
                    stop=False,
                )

        def project_latent(half, r, c):
            matmul_pass(
                banks[("out", half, r, c)],
                ("z%d" % half, 0),
                slice(128 * r, 128 * r + 128),
                ("wz%d" % c, 0),
                start=False,
                stop=True,
            )

        def finish(engine, half, r, c):
            if (half, r) not in rows_out:
                rows_out[(half, r)] = new_slot([P, 1024], F32)
            copy(engine, rows_out[(half, r)][:, 512 * c : 512 * c + 512], banks[("out", half, r, c)][:])

        def store(half, r, c):
            columns = slice(512 * c, 512 * c + 512)
            nc.sync.dma_start(
                out=out[HALF * half : HALF * half + HALF, columns].rearrange("(p r) n -> p r n", r=4)[:, r, :],
                in_=rows_out[(half, r)][:, columns],
            )

        load_scale()
        load_bytes(0)
        load_tokens("h", 0)
        load_bytes(1)
        load_tokens("d", 0)
        for g in range(2):
            load_wq(g)
        for name in ("d", "h"):
            load_tokens(name, 1)
        load_wz()
        load_gain()
        for half in range(2):
            load_eps(half)

        negate_scale()
        for g in range(2):
            for i in range(2):
                transpose_tokens("h", 0, g, i)
        for engine, name in (("S", "rp"), ("V", "px0")):
            widen(engine, name, 0)
        lay_out("S", "px0", 0)
        widen("V", "mp", 0)
        for name in ("rp", "mp"):
            lay_out("V", name, 0)
        for engine, name in (("V", "rp"), ("S", "px1")):
            widen(engine, name, 1)
        for g in range(2):
            for i in range(2):
                copy_tokens("S", "h", 0, g, i)
        for g in range(2):
            for i in range(2):
                transpose_tokens("d", 0, g, i)
        for name in ("rp", "px0"):
            quantize(name, 0)
        lay_out("V", "rp", 1)
        copy_tokens("S", "d", 0, 0, 0)
        widen("S", "mp", 1)
        for g in range(2):
            quantize("h0", g)
        quantize("mp", 0)
        quantize("rp", 1)
        for g, i in ((0, 1), (1, 0), (1, 1)):
            copy_tokens("S", "d", 0, g, i)
        for t in range(4):
            multiply("prior", 0, t)
        for t in range(2):
            sigmoid("prior", 0, t)
        for g in range(2):
            lay_out("V", "rh", g)
        for g in range(2):
            for i in range(2):
                transpose_tokens("d", 1, g, i)
        for t in range(2, 4):
            sigmoid("prior", 0, t)
        for name in ("d0", "rh"):
            for g in range(2):
                quantize(name, g)
        for engine, g, i in (("S", 0, 0), ("V", 0, 1), ("S", 1, 0), ("S", 1, 1)):
            copy_tokens(engine, "d", 1, g, i)
        for t in range(4):
            multiply("up", 0, t)
        widen("V", "px1", 0)
        for t in range(4):
            sigmoid("up", 0, t)
        for name in ("px1", "mp"):
            lay_out("V", name, 1)
        for g in range(2):
            quantize("d1", g)

        for branch, q in (("up", 1), ("prior", 0), ("prior", 1)):
            log_sigmoid(branch, 0, q)
        lay_out("V", "mh", 0)
        for branch, t in (("up", 2), ("up", 3), ("prior", 0), ("prior", 1), ("prior", 2), ("prior", 3)):
            softplus(branch, 0, t)
        widen("V", "px0", 1)
        for g in range(2):
            for i in range(2):
                transpose_tokens("h", 1, g, i)
        log_sigmoid("up", 0, 0)
        for branch, q in (("up", 1), ("prior", 1), ("prior", 0)):
            log_variance(branch, 0, q)
        for t in range(2):
            softplus("up", 0, t)
        for engine, g, i in (("V", 0, 0), ("S", 0, 1), ("V", 1, 0), ("V", 1, 1)):
            copy_tokens(engine, "h", 1, g, i)
        for name, g in (("h1", 0), ("h1", 1), ("mh", 0)):
            quantize(name, g)
        log_variance("up", 0, 0)
        for name in ("up", "prior"):
            for t in range(4):
                multiply(name, 1, t)
        for engine, t in (("V", 0), ("V", 1), ("G", 2), ("G", 3)):
            log_ratio(engine, 0, t)
        for name in ("wz0", "wz1"):
            lay_out("V", name, 0)
        for branch in ("up", "prior"):
            for t in range(4):
                sigmoid(branch, 1, t)
        lay_out("V", "mh", 1)
        for q in range(2):
            weight(0, q)

        log_sigmoid("up", 1, 0)
        for name in ("mp", "mh", "px1"):
            quantize(name, 1)
        for name, g in (("px0", 1), ("px1", 0)):
            lay_out("V", name, g)
        for branch, q in (("up", 1), ("prior", 0), ("prior", 1)):
            log_sigmoid(branch, 1, q)
        for branch in ("up", "prior"):
            for t in range(4):
                softplus(branch, 1, t)

        widen_gain()
        for name in ("diff", "mh"):
            for t in range(4):
                multiply(name, 0, t)
        for name, g in (("wz0", 0), ("px0", 1), ("px1", 0)):
            quantize(name, g)
        for t in range(4):
            shift(0, t)
        for t in range(2):
            mean(0, t)
        for t in range(4):
            merged_variance("G", 0, t)
        for half in range(2):
            for u in range(2):
                transpose_eps(half, u)
        for branch in ("up", "prior"):
            for q in range(2):
                log_variance(branch, 1, q)
        for q in range(2):
            deviation(0, q)
        for t in range(2, 4):
            mean(0, t)
        for name, t in (("diff", 0), ("diff", 1), ("diff", 2), ("mh", 0)):
            multiply(name, 1, t)
        for t in range(4):
            log_ratio("G", 1, t)
        for t in range(4):
            sample(0, t)
        quantize("wz1", 0)
        for name, t in (("diff", 3), ("mh", 1)):
            multiply(name, 1, t)
        for r in range(2):
            latent("V", 0, r)
        for q in range(2):
            weight(1, q)
        for engine, t in (("V", 0), ("G", 1), ("G", 2)):
            merged_variance(engine, 1, t)
        for t in range(4):
            shift(1, t)
        quantize_latent(0, 0)
        for t in range(2, 4):
            multiply("mh", 1, t)
        merged_variance("G", 1, 3)

        for r in range(2):
            project_tokens(0, r, 1)
        for r in range(2):
            project_latent(0, r, 1)
        for t in range(4):
            mean(1, t)
        for q in range(2):
            deviation(1, q)
        for r in range(2):
            project_tokens(0, r, 0)
        for r in (2, 3):
            latent("G", 0, r)
        for t in range(4):
            sample(1, t)
        for r in range(2):
            project_latent(0, r, 0)
        for r in (2, 3):
            for c in range(2):
                project_tokens(0, r, c)
        quantize_latent(0, 1)
        for r in range(2):
            latent("V", 1, r)
        quantize_latent(1, 0)
        for r in (2, 3):
            latent("V", 1, r)
        for r in range(2):
            for c in range(2):
                finish("S", 0, r, c)
        for r in (2, 3):
            for c in range(2):
                project_latent(0, r, c)
        quantize_latent(1, 1)
        for r in (2, 3):
            for c in range(2):
                finish("S", 0, r, c)
        for r in range(4):
            for c in range(2):
                store(0, r, c)

        for r in range(4):
            for c in range(2):
                project_tokens(1, r, c)
                project_latent(1, r, c)
                finish("V", 1, r, c)
                store(1, r, c)
